import numpy as np
import ml_dtypes


def mxq(x, axis, fmt="e4m3"):
    dtype, down = {"e4m3": (ml_dtypes.float8_e4m3fn, 7), "e5m2": (ml_dtypes.float8_e5m2, 14)}[fmt]
    v = np.moveaxis(np.asarray(x, np.float32).astype(ml_dtypes.bfloat16).astype(np.float64), axis, -1)
    blocks = v.reshape(v.shape[:-1] + (-1, 32))
    amax = np.abs(blocks).max(-1, keepdims=True)
    byte = np.maximum(np.where(amax > 0, np.frexp(amax)[1] - 1 + 127, 0) - down, 1)
    scale = np.exp2(byte - 127.0)
    codes = (blocks / scale).astype(np.float32).astype(dtype).astype(np.float64)
    return np.moveaxis((codes * scale).reshape(v.shape), -1, axis)


WIDE = False


def mx_kscale(k):
    if not WIDE:
        return np.ones(k)
    levels = np.array([24, -24, 12, -12, 0])
    if k % 512:
        return np.exp2(np.random.permutation(np.resize(levels, k // 32))).repeat(32)
    a = np.empty((k // 512, 16))
    for p in range(k // 512):
        a[p, :8] = np.random.permutation(np.resize(levels, 8))
        for g in range(8):
            far = levels[np.abs(levels - a[p, g]) >= 10]
            a[p, g + 8] = far[np.random.randint(len(far))]
    return np.exp2(a.ravel()).repeat(32)


def f64(x):
    return np.asarray(x).astype(np.float64)


def striped(idx):
    return np.tile(idx.reshape(-1, 16).T, (8, 1)).astype(np.uint16)


def unstriped(offs):
    return offs[:16].T.reshape(-1).astype(np.int64)


E2M1 = np.array([0.0, 0.5, 1.0, 1.5, 2.0, 3.0, 4.0, 6.0, -0.0, -0.5, -1.0, -1.5, -2.0, -3.0, -4.0, -6.0])


def pack_weight(w, fmt):
    k, n = w.shape
    w = f64(np.asarray(w, np.float32).astype(ml_dtypes.bfloat16)).reshape(k // 32, 32, n)
    amax = np.abs(w).max(1)
    if fmt == "e4m3":
        byte = np.frexp(amax)[1] - 1 + 127 - 7
    else:
        mant, ex = np.frexp(amax / 6.0)
        byte = np.where(mant > 0.5, ex, ex - 1) + 127
    byte = np.clip(np.where(amax > 0, byte, 1), 1, 254)
    scaled = (w * np.exp2(127.0 - byte)[:, None, :]).reshape(k, n).astype(np.float32)
    by_word = np.ascontiguousarray(scaled.reshape(k // 512, 128, 4, n).transpose(0, 1, 3, 2))
    if fmt == "e4m3":
        words = by_word.astype(ml_dtypes.float8_e4m3fn).view(np.uint8)
    else:
        c = by_word.astype(ml_dtypes.float4_e2m1fn).view(np.uint8) & 0xF
        words = (c[..., 0::2] | (c[..., 1::2] << 4)).reshape(k // 512, 128, 2 * n)
    return np.ascontiguousarray(words), np.ascontiguousarray(byte.astype(np.uint8).reshape(k // 512, 16, n))


def unpack_weight(words, scales, fmt):
    g, _, n = scales.shape
    words = np.ascontiguousarray(words).reshape(g, 128, n, -1)
    if fmt == "e4m3":
        vals = words.view(ml_dtypes.float8_e4m3fn).astype(np.float64)
    else:
        nib = np.empty((g, 128, n, 4), np.uint8)
        nib[..., 0::2] = words & 0xF
        nib[..., 1::2] = words >> 4
        vals = E2M1[nib]
    vals = vals * np.repeat(np.exp2(scales.astype(np.float64) - 127.0), 8, axis=1)[..., None]
    return vals.transpose(0, 1, 3, 2).reshape(g * 512, n)


def pack_table4(v):
    words, scales = pack_weight(v, "e2m1")
    g, t = words.shape[0] // 2, v.shape[1]
    return np.ascontiguousarray(words.reshape(g, 2, 128, t, 2).transpose(0, 2, 3, 1, 4).reshape(g, 128, t, 4)), scales


def unpack_table4(words, scales):
    g, _, t, _ = words.shape
    return unpack_weight(words.reshape(g, 128, t, 2, 2).transpose(0, 3, 1, 2, 4).reshape(2 * g, 128, 2 * t), scales, "e2m1")


K, R, M, T, N, J = 1024, 1024, 1024, 2048, 512, 1024


def setup_inputs():
    n = np.random.standard_normal
    u = mx_kscale(R)[:, None]
    s = mx_kscale(K)[:, None]
    x = n((K, M)); x[:512] *= 6.0
    w = n((K, R)) / np.sqrt(K) / s / u.T; w[:512] /= 2.0
    p_w8 = pack_weight(w[:512], "e4m3")
    p_w4 = pack_weight(w[512:], "e2m1")
    p_tab = pack_table4(n((R, T)) * u)
    p_wv4 = pack_weight(n((R, N)) / np.sqrt(R) / u, "e2m1")
    return {
        "x": (x * s).astype(np.float32),
        "w8_words": p_w8[0],
        "w8_scales": p_w8[1],
        "w4_words": p_w4[0],
        "w4_scales": p_w4[1],
        "tab_words": p_tab[0],
        "tab_scales": p_tab[1],
        "wv4_words": p_wv4[0],
        "wv4_scales": p_wv4[1],
        "wvd": (0.4 * (n((R, N)) / np.sqrt(R) / u)).astype(np.float32),
        "offs": striped(np.random.permutation(T)[:J]),
    }


def reference(x, w8_words, w8_scales, w4_words, w4_scales, tab_words, tab_scales, wv4_words, wv4_scales, wvd, offs):
    idx = unstriped(offs)
    x_ = mxq(f64(x), 0, "e4m3")
    w8_ = unpack_weight(w8_words, w8_scales, "e4m3")
    w4_ = unpack_weight(w4_words, w4_scales, "e2m1")
    qa = w8_.T @ x_[:512] + w4_.T @ x_[512:]
    qa_ = mxq(qa, 0, "e4m3")
    tab_ = unpack_table4(tab_words, tab_scales)[:, idx]
    sc = qa_.T @ tab_
    wv4_ = unpack_weight(wv4_words, wv4_scales, "e2m1")
    wvd_ = mxq(f64(wvd), 0, "e4m3")
    vv = wv4_.T @ tab_ + wvd_.T @ tab_
    return np.exp(sc * 0.015625), vv

@@ -1,0 +1,290 @@
+from contextlib import ExitStack
+
+import concourse.mybir as mybir
+
+K, R, M, T, N, J = 1024, 1024, 1024, 2048, 512, 1024
+FLOPS = 2 * K * R * M + 2 * R * M * J + 2 * 2 * R * N * J
+SCORE_SCALE = 0.015625
+
+F32 = mybir.dt.float32
+BF16 = mybir.dt.bfloat16
+I32 = mybir.dt.int32
+U32 = mybir.dt.uint32
+U16 = mybir.dt.uint16
+U8 = mybir.dt.uint8
+FP8X4 = mybir.dt.float8_e4m3fn_x4
+FP4X4 = mybir.dt.float4_e2m1fn_x4
+COPY = mybir.ActivationFunctionType.Copy
+EXP = mybir.ActivationFunctionType.Exp
+
+P = 128
+PACK = 4
+K_PASS = P * PACK
+PASSES = 2
+BANK = 512
+UNIT = 256
+X_CHUNKS = (256, 256, 512)
+ROWS = 4
+
+
+def tile_list_mlat_outl_dl_exp_kernel(
+    tc, x, w8_words, w8_scales, w4_words, w4_scales, tab_words, tab_scales, wv4_words, wv4_scales, wvd, offs, out_0, out_1
+):
+    nc = tc.nc
+    with ExitStack() as ctx:
+        lists = ctx.enter_context(tc.tile_pool(name="lists", bufs=1))
+        keep = ctx.enter_context(tc.tile_pool(name="keep", bufs=1))
+        psum = ctx.enter_context(tc.psum_pool(name="psum", bufs=1))
+
+        def sb(name, shape, dtype, slot=None):
+            return keep.tile(shape, dtype, name=name, tag=slot or name, align_bytes=64)
+
+        banks = [psum.tile([P, BANK], F32, name="bank%d" % b) for b in range(8)]
+        taken = []
+
+        def next_bank():
+            taken.append(len(taken) % len(banks))
+            return banks[taken[-1]]
+
+        def copy_on(on_scalar, dst, src):
+            if on_scalar:
+                nc.scalar.activation(out=dst, in_=src, func=COPY)
+            else:
+                nc.vector.tensor_copy(out=dst, in_=src)
+
+        offsets = lists.tile([P, J // 16], U16, name="offsets")
+        tab_sc = sb("tab_sc", [P, T], U8)
+        tab_w = sb("tab_w", [P, T], I32)
+        plane1 = sb("plane1", [P, J], U8)
+        wv4_w = sb("wv4_w", [P, PASSES, 2 * N], U8)
+        wv4_sc = sb("wv4_sc", [P, PASSES, N], U8)
+        w8_raw = sb("w8_raw", [P, R], I32)
+        w4_raw = sb("w4_raw", [P, 2 * R], U8)
+        w_sc_raw = sb("w_sc_raw", [P, R], U8)
+
+        nc.vector.memset(tab_sc[:].bitcast(I32), 0)
+        nc.vector.memset(plane1[:].bitcast(I32), 0)
+        zero = sb("zero", [P, 1], F32)
+        nc.vector.memset(zero[:], 0.0)
+        nc.gpsimd.memset(wv4_sc[:].rearrange("p a n -> p (a n)").bitcast(I32), 0)
+        nc.gpsimd.memset(w_sc_raw[:].bitcast(I32), 0)
+
+        def load_rows(name, src, a, c0, width):
+            raw = sb(name, [P, PACK, width], F32)
+            rows = src[a * K_PASS : (a + 1) * K_PASS, c0 : c0 + width]
+            nc.sync.dma_start(out=raw[:], in_=rows.rearrange("(p i) c -> p i c", i=PACK))
+            return raw
+
+        nc.sync.dma_start(offsets[:], offs)
+        for q in range(4):
+            nc.scalar.dma_start(
+                out=tab_sc[32 * q : 32 * q + PASSES * ROWS, :].bitcast(I32),
+                in_=tab_scales[:, ROWS * q : ROWS * (q + 1), :].bitcast(I32),
+            )
+        no_bias = sb("no_bias", [P, 1], F32)
+        nc.scalar.activation(out=no_bias[:], in_=zero[:], func=COPY)
+        nc.sync.dma_start(out=tab_w[:], in_=tab_words[0].rearrange("p t b -> p (t b)").bitcast(I32))
+        nc.sync.dma_start(out=wv4_w[:].bitcast(I32), in_=wv4_words.rearrange("a p c -> p a c").bitcast(I32))
+        for q in range(4):
+            nc.gpsimd.dma_start(
+                out=wv4_sc[32 * q : 32 * q + ROWS].bitcast(I32),
+                in_=wv4_scales[:, ROWS * q : ROWS * (q + 1), :].rearrange("a r c -> r a c").bitcast(I32),
+            )
+        for q in range(4):
+            for src, row in ((w4_scales, 0), (w8_scales, ROWS)):
+                nc.gpsimd.dma_start(
+                    out=w_sc_raw[32 * q + row : 32 * q + row + ROWS, :].bitcast(I32),
+                    in_=src[0, ROWS * q : ROWS * (q + 1), :].bitcast(I32),
+                )
+        wvd_raw = [load_rows("wvd_raw%d" % a, wvd, a, 0, N) for a in range(PASSES)]
+        nc.sync.dma_start(out=w8_raw[:], in_=w8_words[0].rearrange("p r b -> p (r b)").bitcast(I32))
+        nc.sync.dma_start(out=w4_raw[:].bitcast(I32), in_=w4_words[0].bitcast(I32))
+        x_raw = {}
+        c0 = 0
+        for width in X_CHUNKS:
+            for a in range(PASSES):
+                raw = load_rows("x_raw%d_%d" % (a, c0), x, a, c0, width)
+                for u in range(width // UNIT):
+                    x_raw[a, c0 // UNIT + u] = raw[:, :, u * UNIT : (u + 1) * UNIT]
+            c0 += width
+
+        def interleave(name, raw, on_scalar, slot=None):
+            grouped = sb(name, [P, UNIT * PACK], BF16, slot=slot)
+            copy_on(
+                on_scalar,
+                grouped[:].rearrange("p (c j i) -> p c i j", j=4, i=PACK),
+                raw.rearrange("p i (c j) -> p c i j", j=4),
+            )
+            return grouped
+
+        def quantize(name, grouped, cols):
+            codes = sb(name + "_codes", [P, cols], U32)
+            scales = sb(name + "_scales", [P, cols], U8)
+            nc.vector.quantize_mx(out=codes[:].bitcast(FP8X4), scales=scales[:], in_=grouped)
+            return codes, scales
+
+        plane0 = sb("plane0", [P, J], U8)
+        tab_planes = [plane0, plane1]
+        tab_codes = {}
+
+        def gather_scales():
+            nc.vector.tensor_copy(plane0[:], tab_sc[:].indirect(offsets[:]))
+            for q in range(4):
+                nc.scalar.dma_start(
+                    out=plane1[32 * q : 32 * q + ROWS, :].bitcast(I32),
+                    in_=plane0[32 * q + ROWS : 32 * q + 2 * ROWS, :].bitcast(I32),
+                )
+
+        def gather_words(h):
+            both = sb("tab_both%d" % h, [P, BANK], I32, slot="tab_both")
+            nc.vector.tensor_copy(both[:].bitcast(U32), tab_w[:].bitcast(U32).indirect(offsets[:, 32 * h : 32 * (h + 1)]))
+            parted = sb("tab_parted%d" % h, [P, PASSES * 2 * BANK], U8)
+            nc.vector.tensor_copy(
+                out=parted[:].bitcast(U16).rearrange("p (a j) -> p a j", a=PASSES),
+                in_=both[:].bitcast(U16).rearrange("p (j a) -> p a j", a=PASSES),
+            )
+            for a in range(PASSES):
+                tab_codes[a, h] = parted[:, a * 2 * BANK : (a + 1) * 2 * BANK].bitcast(FP4X4)
+
+        def with_table(out, codes, scales, a, h, start, stop):
+            nc.tensor.matmul_mx(
+                out=out,
+                lhsT=codes,
+                lhsT_scale=scales,
+                rhs=tab_codes[a, h],
+                rhs_scale=tab_planes[a][:, h * BANK : (h + 1) * BANK],
+                start=start,
+                stop=stop,
+            )
+
+        wvd_q = {}
+
+        def prepare_wvd(a, g):
+            grouped = interleave("wvd_bf%d%d" % (a, g), wvd_raw[a][:, :, g * UNIT : (g + 1) * UNIT], True)
+            wvd_q[a, g] = quantize("wvd%d%d" % (a, g), grouped[:], UNIT)
+
+        vv_bank = {(nt, h): next_bank() for nt in range(N // P) for h in range(2)}
+
+        def vv_base(a, h):
+            for nt in range(N // P):
+                codes = wv4_w[:, a, 2 * P * nt : 2 * P * (nt + 1)].bitcast(FP4X4)
+                with_table(vv_bank[nt, h][:], codes, wv4_sc[:, a, P * nt : P * (nt + 1)], a, h, a == 0, False)
+
+        def vv_delta(a, nt):
+            codes, scales = wvd_q[a, nt // 2]
+            cols = slice(P * (nt % 2), P * (nt % 2 + 1))
+            for h in range(2):
+                with_table(vv_bank[nt, h][:], codes[:, cols].bitcast(FP8X4), scales[:, cols], a, h, False, a == PASSES - 1)
+
+        def vv_store(nt, engines):
+            res = sb("vv_res%d" % nt, [P, J], F32)
+            for h in range(2):
+                copy_on(engines[h], res[:, h * BANK : (h + 1) * BANK], vv_bank[nt, h][:])
+            nc.sync.dma_start(out=out_1[P * nt : P * (nt + 1), :], in_=res[:])
+
+        w8_p = sb("w8_p", [P, R], I32)
+        w4_p = sb("w4_p", [P, 2 * R], U8)
+
+        def permute_w():
+            w_sc = sb("w_sc", [P, R], U8, slot="wvd_bf00")
+            nc.vector.tensor_copy(
+                out=w_sc[:].rearrange("p (a i m) -> p a i m", a=PASSES, i=PACK),
+                in_=w_sc_raw[:].rearrange("p (a m i) -> p a i m", a=PASSES, i=PACK),
+            )
+            for a in range(PASSES):
+                cols = slice(a * K_PASS, (a + 1) * K_PASS)
+                nc.vector.tensor_copy(
+                    out=w8_p[:, cols].rearrange("p (i c j) -> p c i j", i=PACK, j=4),
+                    in_=w8_raw[:, cols].rearrange("p (c j i) -> p c i j", i=PACK, j=4),
+                )
+            nc.vector.tensor_copy(
+                out=w4_p[:].bitcast(U16).rearrange("p (a i m) -> p a i m", a=PASSES, i=PACK),
+                in_=w4_raw[:].bitcast(U16).rearrange("p (a m i) -> p a i m", a=PASSES, i=PACK),
+            )
+            return w_sc
+
+        x_q = {}
+
+        def prepare_x(u, engines, slots):
+            grouped = [interleave("x_bf%d_%d" % (a, u), x_raw[a, u], engines[a], slots[a]) for a in range(PASSES)]
+            for a in range(PASSES):
+                x_q[a, u] = quantize("x%d_%d" % (a, u), grouped[a][:], UNIT)
+
+        qa_q = {}
+
+        def project(mt):
+            cols = slice(P * (mt % 2), P * (mt % 2 + 1))
+            (x8, x8_sc), (x4, x4_sc) = x_q[0, mt // 2], x_q[1, mt // 2]
+            grouped = []
+            for a in range(PASSES):
+                bank = next_bank()
+                for i in range(PACK):
+                    c = a * K_PASS + i * P
+                    nc.tensor.matmul_mx(
+                        out=bank[:, i * P : (i + 1) * P],
+                        lhsT=w8_p[:, c : c + P].bitcast(FP8X4),
+                        lhsT_scale=w_sc[ROWS:P, c : c + P],
+                        rhs=x8[:, cols].bitcast(FP8X4),
+                        rhs_scale=x8_sc[:, cols],
+                        start=True,
+                        stop=False,
+                    )
+                    nc.tensor.matmul_mx(
+                        out=bank[:, i * P : (i + 1) * P],
+                        lhsT=w4_p[:, 2 * c : 2 * (c + P)].bitcast(FP4X4),
+                        lhsT_scale=w_sc[:, c : c + P],
+                        rhs=x4[:, cols].bitcast(FP8X4),
+                        rhs_scale=x4_sc[:, cols],
+                        start=False,
+                        stop=True,
+                    )
+                qa_bf = sb("qa_bf%d_%d" % (a, mt), [P, K_PASS], BF16)
+                copy_on(a == 0, qa_bf[:].rearrange("p (m i) -> p m i", i=PACK), bank[:].rearrange("p (i m) -> p m i", i=PACK))
+                grouped.append(qa_bf)
+            for a in range(PASSES):
+                qa_q[a, mt] = quantize("qa%d_%d" % (a, mt), grouped[a][:], P)
+
+        def score(mt, split_store):
+            pair = [next_bank(), next_bank()]
+            order = [(a, h) for h in range(2) for a in range(PASSES)] if split_store else [(a, h) for a in range(PASSES) for h in range(2)]
+            for a, h in order:
+                codes, scales = qa_q[a, mt]
+                with_table(pair[h][:], codes[:].bitcast(FP8X4), scales[:], a, h, a == 0, a == PASSES - 1)
+            res = sb("sc_res%d" % mt, [P, J], F32)
+            rows = slice(P * mt, P * (mt + 1))
+            for h in range(2):
+                cols = slice(h * BANK, (h + 1) * BANK)
+                nc.scalar.activation(out=res[:, cols], in_=pair[h][:], func=EXP, bias=no_bias[:], scale=SCORE_SCALE)
+                if split_store:
+                    nc.sync.dma_start(out=out_0[rows, cols], in_=res[:, cols])
+            if not split_store:
+                nc.sync.dma_start(out=out_0[rows, :], in_=res[:])
+
+        gather_scales()
+        gather_words(0)
+        vv_base(0, 0)
+        vv_base(1, 0)
+        gather_words(1)
+        vv_base(0, 1)
+        vv_base(1, 1)
+        for g in range(2):
+            for a in range(PASSES):
+                prepare_wvd(a, g)
+        w_sc = permute_w()
+        for nt in range(4):
+            for a in range(PASSES):
+                vv_delta(a, nt)
+        prepare_x(0, (True, False), (None, None))
+        vv_store(0, (True, True))
+        vv_store(1, (True, True))
+        tiles = M // P
+        project(0)
+        vv_store(2, (True, True))
+        vv_store(3, (True, True))
+        for mt in range(1, tiles):
+            if mt % 2 == 1 and mt + 1 < tiles:
+                u = (mt + 1) // 2
+                prepare_x(u, (False, False), ("qa_bf0_%d" % (mt - 1), "qa_bf1_%d" % (mt - 1)) if u > 1 else (None, None))
+            project(mt)
+            score(mt - 1, mt - 1 >= tiles - 2)
+        score(tiles - 1, True)

@@ -86,19 +86,28 @@ def tile_list_mlat_outl_dl_exp_kernel(
         nc.sync.dma_start(out=tab_w[:], in_=tab_words[0].rearrange("p t b -> p (t b)").bitcast(I32))
         nc.sync.dma_start(out=wv4_w[:].bitcast(I32), in_=wv4_words.rearrange("a p c -> p a c").bitcast(I32))
         for q in range(4):
-            nc.gpsimd.dma_start(
+            nc.scalar.dma_start(
                 out=wv4_sc[32 * q : 32 * q + ROWS].bitcast(I32),
                 in_=wv4_scales[:, ROWS * q : ROWS * (q + 1), :].rearrange("a r c -> r a c").bitcast(I32),
             )
-        for q in range(4):
-            for src, row in ((w4_scales, 0), (w8_scales, ROWS)):
-                nc.gpsimd.dma_start(
-                    out=w_sc_raw[32 * q + row : 32 * q + row + ROWS, :].bitcast(I32),
-                    in_=src[0, ROWS * q : ROWS * (q + 1), :].bitcast(I32),
-                )
-        wvd_raw = [load_rows("wvd_raw%d" % a, wvd, a, 0, N) for a in range(PASSES)]
+
+        def load_w_scales(src, row, q):
+            nc.sync.dma_start(
+                out=w_sc_raw[32 * q + row : 32 * q + row + ROWS, :].bitcast(I32),
+                in_=src[0, ROWS * q : ROWS * (q + 1), :].bitcast(I32),
+            )
+
+        wvd_raw = []
+        for a in range(PASSES):
+            wvd_raw.append(load_rows("wvd_raw%d" % a, wvd, a, 0, N))
+            for q in range(2 * a, 2 * a + 2):
+                load_w_scales(w4_scales, 0, q)
         nc.sync.dma_start(out=w8_raw[:], in_=w8_words[0].rearrange("p r b -> p (r b)").bitcast(I32))
+        for q in range(2):
+            load_w_scales(w8_scales, ROWS, q)
         nc.sync.dma_start(out=w4_raw[:].bitcast(I32), in_=w4_words[0].bitcast(I32))
+        for q in range(2, 4):
+            load_w_scales(w8_scales, ROWS, q)
         x_raw = {}
         c0 = 0
         for width in X_CHUNKS:
@@ -182,10 +191,9 @@ def tile_list_mlat_outl_dl_exp_kernel(
                 copy_on(engines[h], res[:, h * BANK : (h + 1) * BANK], vv_bank[nt, h][:])
             nc.sync.dma_start(out=out_1[P * nt : P * (nt + 1), :], in_=res[:])
 
-        w8_p = sb("w8_p", [P, R], I32)
-        w4_p = sb("w4_p", [P, 2 * R], U8)
-
         def permute_w():
+            w8_p = sb("w8_p", [P, R], I32, slot="wvd_bf10")
+            w4_p = sb("w4_p", [P, 2 * R], U8, slot="wvd_bf01")
             w_sc = sb("w_sc", [P, R], U8, slot="wvd_bf00")
             nc.vector.tensor_copy(
                 out=w_sc[:].rearrange("p (a i m) -> p a i m", a=PASSES, i=PACK),
@@ -201,7 +209,7 @@ def tile_list_mlat_outl_dl_exp_kernel(
                 out=w4_p[:].bitcast(U16).rearrange("p (a i m) -> p a i m", a=PASSES, i=PACK),
                 in_=w4_raw[:].bitcast(U16).rearrange("p (a m i) -> p a i m", a=PASSES, i=PACK),
             )
-            return w_sc
+            return w8_p, w4_p, w_sc
 
         x_q = {}
 
@@ -270,11 +278,11 @@ def tile_list_mlat_outl_dl_exp_kernel(
         for g in range(2):
             for a in range(PASSES):
                 prepare_wvd(a, g)
-        w_sc = permute_w()
+        w8_p, w4_p, w_sc = permute_w()
         for nt in range(4):
             for a in range(PASSES):
                 vv_delta(a, nt)
-        prepare_x(0, (True, False), (None, None))
+        prepare_x(0, (False, False), (None, None))
         vv_store(0, (True, True))
         vv_store(1, (True, True))
         tiles = M // P

@@ -77,19 +77,19 @@ def tile_list_mlat_outl_dl_exp_kernel(
 
         nc.sync.dma_start(offsets[:], offs)
         for q in range(4):
-            nc.scalar.dma_start(
+            nc.sync.dma_start(
                 out=tab_sc[32 * q : 32 * q + PASSES * ROWS, :].bitcast(I32),
                 in_=tab_scales[:, ROWS * q : ROWS * (q + 1), :].bitcast(I32),
             )
         no_bias = sb("no_bias", [P, 1], F32)
         nc.scalar.activation(out=no_bias[:], in_=zero[:], func=COPY)
         nc.sync.dma_start(out=tab_w[:], in_=tab_words[0].rearrange("p t b -> p (t b)").bitcast(I32))
-        nc.sync.dma_start(out=wv4_w[:].bitcast(I32), in_=wv4_words.rearrange("a p c -> p a c").bitcast(I32))
         for q in range(4):
             nc.scalar.dma_start(
                 out=wv4_sc[32 * q : 32 * q + ROWS].bitcast(I32),
                 in_=wv4_scales[:, ROWS * q : ROWS * (q + 1), :].rearrange("a r c -> r a c").bitcast(I32),
             )
+        nc.sync.dma_start(out=wv4_w[:].bitcast(I32), in_=wv4_words.rearrange("a p c -> p a c").bitcast(I32))
 
         def load_w_scales(src, row, q):
             nc.sync.dma_start(
@@ -174,10 +174,9 @@ def tile_list_mlat_outl_dl_exp_kernel(
 
         vv_bank = {(nt, h): next_bank() for nt in range(N // P) for h in range(2)}
 
-        def vv_base(a, h):
-            for nt in range(N // P):
-                codes = wv4_w[:, a, 2 * P * nt : 2 * P * (nt + 1)].bitcast(FP4X4)
-                with_table(vv_bank[nt, h][:], codes, wv4_sc[:, a, P * nt : P * (nt + 1)], a, h, a == 0, False)
+        def vv_base(a, nt, h):
+            codes = wv4_w[:, a, 2 * P * nt : 2 * P * (nt + 1)].bitcast(FP4X4)
+            with_table(vv_bank[nt, h][:], codes, wv4_sc[:, a, P * nt : P * (nt + 1)], a, h, a == 0, False)
 
         def vv_delta(a, nt):
             codes, scales = wvd_q[a, nt // 2]
@@ -213,39 +212,35 @@ def tile_list_mlat_outl_dl_exp_kernel(
 
         x_q = {}
 
-        def prepare_x(u, engines, slots):
-            grouped = [interleave("x_bf%d_%d" % (a, u), x_raw[a, u], engines[a], slots[a]) for a in range(PASSES)]
-            for a in range(PASSES):
-                x_q[a, u] = quantize("x%d_%d" % (a, u), grouped[a][:], UNIT)
+        def prepare_x(a, u, slot):
+            grouped = interleave("x_bf%d_%d" % (a, u), x_raw[a, u], False, slot)
+            x_q[a, u] = quantize("x%d_%d" % (a, u), grouped[:], UNIT)
 
         qa_q = {}
 
         def project(mt):
             cols = slice(P * (mt % 2), P * (mt % 2 + 1))
-            (x8, x8_sc), (x4, x4_sc) = x_q[0, mt // 2], x_q[1, mt // 2]
             grouped = []
             for a in range(PASSES):
                 bank = next_bank()
-                for i in range(PACK):
-                    c = a * K_PASS + i * P
-                    nc.tensor.matmul_mx(
-                        out=bank[:, i * P : (i + 1) * P],
-                        lhsT=w8_p[:, c : c + P].bitcast(FP8X4),
-                        lhsT_scale=w_sc[ROWS:P, c : c + P],
-                        rhs=x8[:, cols].bitcast(FP8X4),
-                        rhs_scale=x8_sc[:, cols],
-                        start=True,
-                        stop=False,
-                    )
-                    nc.tensor.matmul_mx(
-                        out=bank[:, i * P : (i + 1) * P],
-                        lhsT=w4_p[:, 2 * c : 2 * (c + P)].bitcast(FP4X4),
-                        lhsT_scale=w_sc[:, c : c + P],
-                        rhs=x4[:, cols].bitcast(FP8X4),
-                        rhs_scale=x4_sc[:, cols],
-                        start=False,
-                        stop=True,
-                    )
+                order = (0, 1) if a == 0 else (1, 0)
+                for kp in order:
+                    for i in range(PACK):
+                        c = a * K_PASS + i * P
+                        if kp == 0:
+                            w_codes, w_plane = w8_p[:, c : c + P].bitcast(FP8X4), w_sc[ROWS:P, c : c + P]
+                        else:
+                            w_codes, w_plane = w4_p[:, 2 * c : 2 * (c + P)].bitcast(FP4X4), w_sc[:, c : c + P]
+                        x_codes, x_plane = x_q[kp, mt // 2]
+                        nc.tensor.matmul_mx(
+                            out=bank[:, i * P : (i + 1) * P],
+                            lhsT=w_codes,
+                            lhsT_scale=w_plane,
+                            rhs=x_codes[:, cols].bitcast(FP8X4),
+                            rhs_scale=x_plane[:, cols],
+                            start=(kp == order[0] and i == 0),
+                            stop=(kp == order[1] and i == PACK - 1),
+                        )
                 qa_bf = sb("qa_bf%d_%d" % (a, mt), [P, K_PASS], BF16)
                 copy_on(a == 0, qa_bf[:].rearrange("p (m i) -> p m i", i=PACK), bank[:].rearrange("p (i m) -> p m i", i=PACK))
                 grouped.append(qa_bf)
@@ -269,20 +264,23 @@ def tile_list_mlat_outl_dl_exp_kernel(
                 nc.sync.dma_start(out=out_0[rows, :], in_=res[:])
 
         gather_scales()
-        gather_words(0)
-        vv_base(0, 0)
-        vv_base(1, 0)
-        gather_words(1)
-        vv_base(0, 1)
-        vv_base(1, 1)
-        for g in range(2):
-            for a in range(PASSES):
+        for h in range(2):
+            gather_words(h)
+            for nt in range(4):
+                vv_base(0, nt, h)
+        for a in range(PASSES):
+            for g in range(2):
                 prepare_wvd(a, g)
+        for nt in range(4):
+            vv_delta(0, nt)
         w8_p, w4_p, w_sc = permute_w()
         for nt in range(4):
-            for a in range(PASSES):
-                vv_delta(a, nt)
-        prepare_x(0, (False, False), (None, None))
+            for h in range(2):
+                vv_base(1, nt, h)
+            vv_delta(1, nt)
+        prepare_x(0, 0, None)
+        prepare_x(1, 0, None)
+        prepare_x(0, 1, None)
         vv_store(0, (True, True))
         vv_store(1, (True, True))
         tiles = M // P
@@ -290,9 +288,9 @@ def tile_list_mlat_outl_dl_exp_kernel(
         vv_store(2, (True, True))
         vv_store(3, (True, True))
         for mt in range(1, tiles):
-            if mt % 2 == 1 and mt + 1 < tiles:
-                u = (mt + 1) // 2
-                prepare_x(u, (False, False), ("qa_bf0_%d" % (mt - 1), "qa_bf1_%d" % (mt - 1)) if u > 1 else (None, None))
+            a, u = mt % 2, (mt + 2) // 2
+            if u < M // UNIT:
+                prepare_x(a, u, "qa_bf1_%d" % (mt - 1))
             project(mt)
             score(mt - 1, mt - 1 >= tiles - 2)
         score(tiles - 1, True)

@@ -23,8 +23,9 @@ K_PASS = P * PACK
 PASSES = 2
 BANK = 512
 UNIT = 256
-X_CHUNKS = (256, 256, 512)
+X_CHUNKS = (256, 256, 256, 256)
 ROWS = 4
+EARLY = 7
 
 
 def tile_list_mlat_outl_dl_exp_kernel(
@@ -75,21 +76,24 @@ def tile_list_mlat_outl_dl_exp_kernel(
             nc.sync.dma_start(out=raw[:], in_=rows.rearrange("(p i) c -> p i c", i=PACK))
             return raw
 
-        nc.sync.dma_start(offsets[:], offs)
-        for q in range(4):
-            nc.sync.dma_start(
-                out=tab_sc[32 * q : 32 * q + PASSES * ROWS, :].bitcast(I32),
-                in_=tab_scales[:, ROWS * q : ROWS * (q + 1), :].bitcast(I32),
-            )
-        no_bias = sb("no_bias", [P, 1], F32)
-        nc.scalar.activation(out=no_bias[:], in_=zero[:], func=COPY)
-        nc.sync.dma_start(out=tab_w[:], in_=tab_words[0].rearrange("p t b -> p (t b)").bitcast(I32))
-        for q in range(4):
+        def load_wv4_scales(q):
             nc.scalar.dma_start(
                 out=wv4_sc[32 * q : 32 * q + ROWS].bitcast(I32),
                 in_=wv4_scales[:, ROWS * q : ROWS * (q + 1), :].rearrange("a r c -> r a c").bitcast(I32),
             )
-        nc.sync.dma_start(out=wv4_w[:].bitcast(I32), in_=wv4_words.rearrange("a p c -> p a c").bitcast(I32))
+
+        nc.sync.dma_start(offsets[:], offs)
+        for q in range(4):
+            nc.scalar.dma_start(
+                out=tab_sc[32 * q : 32 * q + PASSES * ROWS, :].bitcast(I32),
+                in_=tab_scales[:, ROWS * q : ROWS * (q + 1), :].bitcast(I32),
+            )
+        load_wv4_scales(0)
+        no_bias = sb("no_bias", [P, 1], F32)
+        nc.scalar.activation(out=no_bias[:], in_=zero[:], func=COPY)
+        nc.sync.dma_start(out=tab_w[:], in_=tab_words[0].rearrange("p t b -> p (t b)").bitcast(I32))
+        for q in range(1, 4):
+            load_wv4_scales(q)
 
         def load_w_scales(src, row, q):
             nc.sync.dma_start(
@@ -97,28 +101,30 @@ def tile_list_mlat_outl_dl_exp_kernel(
                 in_=src[0, ROWS * q : ROWS * (q + 1), :].bitcast(I32),
             )
 
-        wvd_raw = []
-        for a in range(PASSES):
-            wvd_raw.append(load_rows("wvd_raw%d" % a, wvd, a, 0, N))
-            for q in range(2 * a, 2 * a + 2):
-                load_w_scales(w4_scales, 0, q)
+        wvd_raw = {}
+        nc.sync.dma_start(out=wv4_w[:].bitcast(I32), in_=wv4_words.rearrange("a p c -> p a c").bitcast(I32))
+        wvd_raw[0] = load_rows("wvd_raw0", wvd, 0, 0, N)
+        wvd_raw[1] = load_rows("wvd_raw1", wvd, 1, 0, N)
         nc.sync.dma_start(out=w8_raw[:], in_=w8_words[0].rearrange("p r b -> p (r b)").bitcast(I32))
-        for q in range(2):
-            load_w_scales(w8_scales, ROWS, q)
         nc.sync.dma_start(out=w4_raw[:].bitcast(I32), in_=w4_words[0].bitcast(I32))
-        for q in range(2, 4):
-            load_w_scales(w8_scales, ROWS, q)
+        load_w_scales(w4_scales, 0, 0)
+        load_w_scales(w4_scales, 0, 1)
+        load_w_scales(w4_scales, 0, 2)
+        load_w_scales(w4_scales, 0, 3)
         x_raw = {}
         c0 = 0
         for width in X_CHUNKS:
             for a in range(PASSES):
                 raw = load_rows("x_raw%d_%d" % (a, c0), x, a, c0, width)
+                if c0 == 0 and a == 0:
+                    for q in range(0, 4):
+                        load_w_scales(w8_scales, ROWS, q)
                 for u in range(width // UNIT):
                     x_raw[a, c0 // UNIT + u] = raw[:, :, u * UNIT : (u + 1) * UNIT]
             c0 += width
 
-        def interleave(name, raw, on_scalar, slot=None):
-            grouped = sb(name, [P, UNIT * PACK], BF16, slot=slot)
+        def interleave(name, raw, on_scalar):
+            grouped = sb(name, [P, raw.shape[2] * PACK], BF16)
             copy_on(
                 on_scalar,
                 grouped[:].rearrange("p (c j i) -> p c i j", j=4, i=PACK),
@@ -138,6 +144,8 @@ def tile_list_mlat_outl_dl_exp_kernel(
 
         def gather_scales():
             nc.vector.tensor_copy(plane0[:], tab_sc[:].indirect(offsets[:]))
+
+        def move_scales():
             for q in range(4):
                 nc.scalar.dma_start(
                     out=plane1[32 * q : 32 * q + ROWS, :].bitcast(I32),
@@ -145,15 +153,20 @@ def tile_list_mlat_outl_dl_exp_kernel(
                 )
 
         def gather_words(h):
-            both = sb("tab_both%d" % h, [P, BANK], I32, slot="tab_both")
-            nc.vector.tensor_copy(both[:].bitcast(U32), tab_w[:].bitcast(U32).indirect(offsets[:, 32 * h : 32 * (h + 1)]))
-            parted = sb("tab_parted%d" % h, [P, PASSES * 2 * BANK], U8)
-            nc.vector.tensor_copy(
-                out=parted[:].bitcast(U16).rearrange("p (a j) -> p a j", a=PASSES),
-                in_=both[:].bitcast(U16).rearrange("p (j a) -> p a j", a=PASSES),
-            )
+            pieces = []
+            for c0 in range(0, BANK, UNIT):
+                both = sb("tab_both%d_%d" % (h, c0), [P, UNIT], I32)
+                listed = offsets[:, (h * BANK + c0) // 16 : (h * BANK + c0 + UNIT) // 16]
+                nc.vector.tensor_copy(both[:].bitcast(U32), tab_w[:].bitcast(U32).indirect(listed))
+                pieces.append((c0, both))
+            parted = [sb("tab_parted%d%d" % (a, h), [P, 2 * BANK], U8) for a in range(PASSES)]
+            for c0, both in pieces:
+                for a in range(PASSES):
+                    nc.vector.tensor_copy(
+                        out=parted[a][:].bitcast(U16)[:, c0 : c0 + UNIT], in_=both[:].bitcast(U16)[:, a :: PASSES]
+                    )
             for a in range(PASSES):
-                tab_codes[a, h] = parted[:, a * 2 * BANK : (a + 1) * 2 * BANK].bitcast(FP4X4)
+                tab_codes[a, h] = parted[a][:].bitcast(FP4X4)
 
         def with_table(out, codes, scales, a, h, start, stop):
             nc.tensor.matmul_mx(
@@ -172,28 +185,40 @@ def tile_list_mlat_outl_dl_exp_kernel(
             grouped = interleave("wvd_bf%d%d" % (a, g), wvd_raw[a][:, :, g * UNIT : (g + 1) * UNIT], True)
             wvd_q[a, g] = quantize("wvd%d%d" % (a, g), grouped[:], UNIT)
 
-        vv_bank = {(nt, h): next_bank() for nt in range(N // P) for h in range(2)}
+        early = [(nt, h) for nt in range(N // P) for h in range(2)][:EARLY]
+        vv_bank = {key: next_bank() for key in early}
 
         def vv_base(a, nt, h):
             codes = wv4_w[:, a, 2 * P * nt : 2 * P * (nt + 1)].bitcast(FP4X4)
             with_table(vv_bank[nt, h][:], codes, wv4_sc[:, a, P * nt : P * (nt + 1)], a, h, a == 0, False)
 
-        def vv_delta(a, nt):
+        def warm_up(passes):
+            for n in range(passes):
+                nc.tensor.matmul_mx(
+                    out=banks[7][:],
+                    lhsT=wv4_w[:, 0, 0 : 2 * P].bitcast(FP4X4),
+                    lhsT_scale=plane0[:, 0:P],
+                    rhs=wv4_w[:, 0, :].bitcast(FP4X4),
+                    rhs_scale=plane0[:, 0:BANK],
+                    start=True,
+                    stop=True,
+                )
+
+        def vv_delta(a, nt, h):
             codes, scales = wvd_q[a, nt // 2]
             cols = slice(P * (nt % 2), P * (nt % 2 + 1))
-            for h in range(2):
-                with_table(vv_bank[nt, h][:], codes[:, cols].bitcast(FP8X4), scales[:, cols], a, h, False, a == PASSES - 1)
+            with_table(vv_bank[nt, h][:], codes[:, cols].bitcast(FP8X4), scales[:, cols], a, h, False, a == PASSES - 1)
 
-        def vv_store(nt, engines):
-            res = sb("vv_res%d" % nt, [P, J], F32)
-            for h in range(2):
-                copy_on(engines[h], res[:, h * BANK : (h + 1) * BANK], vv_bank[nt, h][:])
-            nc.sync.dma_start(out=out_1[P * nt : P * (nt + 1), :], in_=res[:])
+        def vv_store(nt, halves, on_scalar):
+            res = sb("vv_res%d_%d" % (nt, halves[0]), [P, BANK * len(halves)], F32)
+            for n, h in enumerate(halves):
+                copy_on(on_scalar, res[:, n * BANK : (n + 1) * BANK], vv_bank[nt, h][:])
+            nc.sync.dma_start(out=out_1[P * nt : P * (nt + 1), halves[0] * BANK : (halves[-1] + 1) * BANK], in_=res[:])
 
         def permute_w():
-            w8_p = sb("w8_p", [P, R], I32, slot="wvd_bf10")
-            w4_p = sb("w4_p", [P, 2 * R], U8, slot="wvd_bf01")
-            w_sc = sb("w_sc", [P, R], U8, slot="wvd_bf00")
+            w8_p = sb("w8_p", [P, R], I32)
+            w4_p = sb("w4_p", [P, 2 * R], U8)
+            w_sc = sb("w_sc", [P, R], U8)
             nc.vector.tensor_copy(
                 out=w_sc[:].rearrange("p (a i m) -> p a i m", a=PASSES, i=PACK),
                 in_=w_sc_raw[:].rearrange("p (a m i) -> p a i m", a=PASSES, i=PACK),
@@ -212,14 +237,16 @@ def tile_list_mlat_outl_dl_exp_kernel(
 
         x_q = {}
 
-        def prepare_x(a, u, slot):
-            grouped = interleave("x_bf%d_%d" % (a, u), x_raw[a, u], False, slot)
-            x_q[a, u] = quantize("x%d_%d" % (a, u), grouped[:], UNIT)
+        def prepare_x(a, mt, count, on_scalar):
+            raw = x_raw[a, mt // 2][:, :, P * (mt % 2) : P * (mt % 2 + count)]
+            grouped = interleave("x_bf%d_%d" % (a, mt), raw, on_scalar)
+            codes, scales = quantize("x%d_%d" % (a, mt), grouped[:], P * count)
+            for n in range(count):
+                x_q[a, mt + n] = codes[:, P * n : P * (n + 1)].bitcast(FP8X4), scales[:, P * n : P * (n + 1)]
 
         qa_q = {}
 
-        def project(mt):
-            cols = slice(P * (mt % 2), P * (mt % 2 + 1))
+        def project(mt, engines):
             grouped = []
             for a in range(PASSES):
                 bank = next_bank()
@@ -231,23 +258,23 @@ def tile_list_mlat_outl_dl_exp_kernel(
                             w_codes, w_plane = w8_p[:, c : c + P].bitcast(FP8X4), w_sc[ROWS:P, c : c + P]
                         else:
                             w_codes, w_plane = w4_p[:, 2 * c : 2 * (c + P)].bitcast(FP4X4), w_sc[:, c : c + P]
-                        x_codes, x_plane = x_q[kp, mt // 2]
+                        x_codes, x_plane = x_q[kp, mt]
                         nc.tensor.matmul_mx(
                             out=bank[:, i * P : (i + 1) * P],
                             lhsT=w_codes,
                             lhsT_scale=w_plane,
-                            rhs=x_codes[:, cols].bitcast(FP8X4),
-                            rhs_scale=x_plane[:, cols],
+                            rhs=x_codes,
+                            rhs_scale=x_plane,
                             start=(kp == order[0] and i == 0),
                             stop=(kp == order[1] and i == PACK - 1),
                         )
                 qa_bf = sb("qa_bf%d_%d" % (a, mt), [P, K_PASS], BF16)
-                copy_on(a == 0, qa_bf[:].rearrange("p (m i) -> p m i", i=PACK), bank[:].rearrange("p (i m) -> p m i", i=PACK))
+                copy_on(engines[a], qa_bf[:].rearrange("p (m i) -> p m i", i=PACK), bank[:].rearrange("p (i m) -> p m i", i=PACK))
                 grouped.append(qa_bf)
             for a in range(PASSES):
                 qa_q[a, mt] = quantize("qa%d_%d" % (a, mt), grouped[a][:], P)
 
-        def score(mt, split_store):
+        def score(mt, split_store, pieces=((0, BANK), (BANK, J))):
             pair = [next_bank(), next_bank()]
             order = [(a, h) for h in range(2) for a in range(PASSES)] if split_store else [(a, h) for a in range(PASSES) for h in range(2)]
             for a, h in order:
@@ -255,42 +282,54 @@ def tile_list_mlat_outl_dl_exp_kernel(
                 with_table(pair[h][:], codes[:].bitcast(FP8X4), scales[:], a, h, a == 0, a == PASSES - 1)
             res = sb("sc_res%d" % mt, [P, J], F32)
             rows = slice(P * mt, P * (mt + 1))
-            for h in range(2):
-                cols = slice(h * BANK, (h + 1) * BANK)
-                nc.scalar.activation(out=res[:, cols], in_=pair[h][:], func=EXP, bias=no_bias[:], scale=SCORE_SCALE)
+            for c0, c1 in pieces:
+                h = c0 // BANK
+                nc.scalar.activation(
+                    out=res[:, c0:c1], in_=pair[h][:, c0 - h * BANK : c1 - h * BANK], func=EXP, bias=no_bias[:], scale=SCORE_SCALE
+                )
                 if split_store:
-                    nc.sync.dma_start(out=out_0[rows, cols], in_=res[:, cols])
+                    nc.sync.dma_start(out=out_0[rows, c0:c1], in_=res[:, c0:c1])
             if not split_store:
                 nc.sync.dma_start(out=out_0[rows, :], in_=res[:])
 
         gather_scales()
+        move_scales()
         for h in range(2):
             gather_words(h)
-            for nt in range(4):
-                vv_base(0, nt, h)
-        for a in range(PASSES):
-            for g in range(2):
-                prepare_wvd(a, g)
-        for nt in range(4):
-            vv_delta(0, nt)
+            for nt, hh in early:
+                if hh == h:
+                    vv_base(0, nt, h)
+        for g in range(2):
+            prepare_wvd(0, g)
+        for nt, h in early:
+            vv_delta(0, nt, h)
         w8_p, w4_p, w_sc = permute_w()
+        for g in range(2):
+            prepare_wvd(1, g)
         for nt in range(4):
-            for h in range(2):
-                vv_base(1, nt, h)
-            vv_delta(1, nt)
-        prepare_x(0, 0, None)
-        prepare_x(1, 0, None)
-        prepare_x(0, 1, None)
-        vv_store(0, (True, True))
-        vv_store(1, (True, True))
+            for step in (vv_base, vv_delta):
+                for h in range(2):
+                    if (nt, h) in early:
+                        step(1, nt, h)
+        prepare_x(0, 0, 2, False)
+        prepare_x(1, 0, 1, False)
+        prepare_x(1, 1, 1, False)
+        prepare_x(0, 2, 2, False)
+        vv_store(0, (0, 1), True)
+        vv_store(1, (0, 1), True)
         tiles = M // P
-        project(0)
-        vv_store(2, (True, True))
-        vv_store(3, (True, True))
+        project(0, (True, False))
+        vv_store(2, (0, 1), True)
+        vv_store(3, (0,), True)
         for mt in range(1, tiles):
             a, u = mt % 2, (mt + 2) // 2
             if u < M // UNIT:
-                prepare_x(a, u, "qa_bf1_%d" % (mt - 1))
-            project(mt)
+                prepare_x(a, 2 * u, 2, mt in (1,2,3,4,5))
+            project(mt, (mt in (6, 7), False))
             score(mt - 1, mt - 1 >= tiles - 2)
+        vv_bank[3, 1] = next_bank()
+        for step in (vv_base, vv_delta):
+            for a in range(PASSES):
+                step(a, 3, 1)
+        vv_store(3, (1,), False)
         score(tiles - 1, True)

@@ -23,9 +23,7 @@ K_PASS = P * PACK
 PASSES = 2
 BANK = 512
 UNIT = 256
-X_CHUNKS = (256, 256, 256, 256)
 ROWS = 4
-EARLY = 7
 
 
 def tile_list_mlat_outl_dl_exp_kernel(
@@ -41,11 +39,6 @@ def tile_list_mlat_outl_dl_exp_kernel(
             return keep.tile(shape, dtype, name=name, tag=slot or name, align_bytes=64)
 
         banks = [psum.tile([P, BANK], F32, name="bank%d" % b) for b in range(8)]
-        taken = []
-
-        def next_bank():
-            taken.append(len(taken) % len(banks))
-            return banks[taken[-1]]
 
         def copy_on(on_scalar, dst, src):
             if on_scalar:
@@ -63,12 +56,13 @@ def tile_list_mlat_outl_dl_exp_kernel(
         w4_raw = sb("w4_raw", [P, 2 * R], U8)
         w_sc_raw = sb("w_sc_raw", [P, R], U8)
 
-        nc.vector.memset(tab_sc[:].bitcast(I32), 0)
-        nc.vector.memset(plane1[:].bitcast(I32), 0)
-        zero = sb("zero", [P, 1], F32)
-        nc.vector.memset(zero[:], 0.0)
+        nc.vector.memset(tab_sc[:, : T // 2].bitcast(I32), 0)
+        nc.gpsimd.memset(tab_sc[:, T // 2 :].bitcast(I32), 0)
         nc.gpsimd.memset(wv4_sc[:].rearrange("p a n -> p (a n)").bitcast(I32), 0)
-        nc.gpsimd.memset(w_sc_raw[:].bitcast(I32), 0)
+        zero = sb("zero", [P, 1], F32)
+        nc.vector.memset(w_sc_raw[:].bitcast(I32), 0)
+        nc.vector.memset(plane1[:].bitcast(I32), 0)
+        nc.vector.memset(zero[:], 0.0)
 
         def load_rows(name, src, a, c0, width):
             raw = sb(name, [P, PACK, width], F32)
@@ -76,24 +70,11 @@ def tile_list_mlat_outl_dl_exp_kernel(
             nc.sync.dma_start(out=raw[:], in_=rows.rearrange("(p i) c -> p i c", i=PACK))
             return raw
 
-        def load_wv4_scales(q):
-            nc.scalar.dma_start(
+        def load_wv4_scales(queue, q):
+            queue.dma_start(
                 out=wv4_sc[32 * q : 32 * q + ROWS].bitcast(I32),
                 in_=wv4_scales[:, ROWS * q : ROWS * (q + 1), :].rearrange("a r c -> r a c").bitcast(I32),
             )
-
-        nc.sync.dma_start(offsets[:], offs)
-        for q in range(4):
-            nc.scalar.dma_start(
-                out=tab_sc[32 * q : 32 * q + PASSES * ROWS, :].bitcast(I32),
-                in_=tab_scales[:, ROWS * q : ROWS * (q + 1), :].bitcast(I32),
-            )
-        load_wv4_scales(0)
-        no_bias = sb("no_bias", [P, 1], F32)
-        nc.scalar.activation(out=no_bias[:], in_=zero[:], func=COPY)
-        nc.sync.dma_start(out=tab_w[:], in_=tab_words[0].rearrange("p t b -> p (t b)").bitcast(I32))
-        for q in range(1, 4):
-            load_wv4_scales(q)
 
         def load_w_scales(src, row, q):
             nc.sync.dma_start(
@@ -102,29 +83,59 @@ def tile_list_mlat_outl_dl_exp_kernel(
             )
 
         wvd_raw = {}
+        x_raw = {}
+
+        def load_wvd(a, g):
+            wvd_raw[a, g] = load_rows("wvd_raw%d_%d" % (a, g), wvd, a, g * UNIT, UNIT)
+
+        def load_x(a, u0, count):
+            raw = load_rows("x_raw%d_%d" % (a, u0), x, a, u0 * UNIT, count * UNIT)
+            for n in range(count):
+                x_raw[a, u0 + n] = raw[:, :, n * UNIT : (n + 1) * UNIT]
+
+        plane0 = sb("plane0", [P, J], U8)
+        tab_planes = [plane0, plane1]
+        tab_codes = {}
+        nc.sync.dma_start(offsets[:], offs)
+        for q in range(4):
+            (nc.sync if q < 2 else nc.scalar).dma_start(
+                out=tab_sc[32 * q : 32 * q + PASSES * ROWS, :].bitcast(I32),
+                in_=tab_scales[:, ROWS * q : ROWS * (q + 1), :].bitcast(I32),
+            )
+        load_wv4_scales(nc.scalar, 0)
+        load_wv4_scales(nc.scalar, 1)
+        no_bias = sb("no_bias", [P, 1], F32)
+        nc.scalar.activation(out=no_bias[:], in_=zero[:], func=COPY)
+        nc.sync.dma_start(out=tab_w[:], in_=tab_words[0].rearrange("p t b -> p (t b)").bitcast(I32))
+        load_wv4_scales(nc.sync, 2)
+        load_wv4_scales(nc.sync, 3)
+        for q in range(2):
+            load_w_scales(w8_scales, ROWS, q)
         nc.sync.dma_start(out=wv4_w[:].bitcast(I32), in_=wv4_words.rearrange("a p c -> p a c").bitcast(I32))
-        wvd_raw[0] = load_rows("wvd_raw0", wvd, 0, 0, N)
-        wvd_raw[1] = load_rows("wvd_raw1", wvd, 1, 0, N)
+        load_wvd(0, 0)
+        load_wvd(1, 0)
+        nc.vector.tensor_copy(plane0[:], tab_sc[:].indirect(offsets[:]))
+        for q in range(4):
+            nc.sync.dma_start(
+                out=plane1[32 * q : 32 * q + ROWS, :].bitcast(I32),
+                in_=plane0[32 * q + ROWS : 32 * q + 2 * ROWS, :].bitcast(I32),
+            )
         nc.sync.dma_start(out=w8_raw[:], in_=w8_words[0].rearrange("p r b -> p (r b)").bitcast(I32))
         nc.sync.dma_start(out=w4_raw[:].bitcast(I32), in_=w4_words[0].bitcast(I32))
-        load_w_scales(w4_scales, 0, 0)
-        load_w_scales(w4_scales, 0, 1)
-        load_w_scales(w4_scales, 0, 2)
-        load_w_scales(w4_scales, 0, 3)
-        x_raw = {}
-        c0 = 0
-        for width in X_CHUNKS:
+        load_w_scales(w8_scales, ROWS, 2)
+        load_x(0, 0, 1)
+        load_w_scales(w8_scales, ROWS, 3)
+        for q in range(4):
+            load_w_scales(w4_scales, 0, q)
+        load_x(1, 0, 1)
+        load_wvd(0, 1)
+        load_wvd(1, 1)
+        for u0, count in ((1, 1), (2, 2)):
             for a in range(PASSES):
-                raw = load_rows("x_raw%d_%d" % (a, c0), x, a, c0, width)
-                if c0 == 0 and a == 0:
-                    for q in range(0, 4):
-                        load_w_scales(w8_scales, ROWS, q)
-                for u in range(width // UNIT):
-                    x_raw[a, c0 // UNIT + u] = raw[:, :, u * UNIT : (u + 1) * UNIT]
-            c0 += width
+                load_x(a, u0, count)
 
         def interleave(name, raw, on_scalar):
-            grouped = sb(name, [P, raw.shape[2] * PACK], BF16)
+            grouped = sb(name, [P, UNIT * PACK], BF16)
             copy_on(
                 on_scalar,
                 grouped[:].rearrange("p (c j i) -> p c i j", j=4, i=PACK),
@@ -135,38 +146,20 @@ def tile_list_mlat_outl_dl_exp_kernel(
         def quantize(name, grouped, cols):
             codes = sb(name + "_codes", [P, cols], U32)
             scales = sb(name + "_scales", [P, cols], U8)
-            nc.vector.quantize_mx(out=codes[:].bitcast(FP8X4), scales=scales[:], in_=grouped)
+            nc.vector.quantize_mx(out=codes[:].bitcast(FP8X4), scales=scales[:], in_=grouped[:])
             return codes, scales
 
-        plane0 = sb("plane0", [P, J], U8)
-        tab_planes = [plane0, plane1]
-        tab_codes = {}
-
-        def gather_scales():
-            nc.vector.tensor_copy(plane0[:], tab_sc[:].indirect(offsets[:]))
-
-        def move_scales():
-            for q in range(4):
-                nc.scalar.dma_start(
-                    out=plane1[32 * q : 32 * q + ROWS, :].bitcast(I32),
-                    in_=plane0[32 * q + ROWS : 32 * q + 2 * ROWS, :].bitcast(I32),
-                )
-
         def gather_words(h):
-            pieces = []
-            for c0 in range(0, BANK, UNIT):
-                both = sb("tab_both%d_%d" % (h, c0), [P, UNIT], I32)
-                listed = offsets[:, (h * BANK + c0) // 16 : (h * BANK + c0 + UNIT) // 16]
-                nc.vector.tensor_copy(both[:].bitcast(U32), tab_w[:].bitcast(U32).indirect(listed))
-                pieces.append((c0, both))
-            parted = [sb("tab_parted%d%d" % (a, h), [P, 2 * BANK], U8) for a in range(PASSES)]
-            for c0, both in pieces:
-                for a in range(PASSES):
-                    nc.vector.tensor_copy(
-                        out=parted[a][:].bitcast(U16)[:, c0 : c0 + UNIT], in_=both[:].bitcast(U16)[:, a :: PASSES]
-                    )
+            both = sb("tab_both%d" % h, [P, BANK], I32, "tab_both")
+            listed = offsets[:, h * BANK // 16 : (h + 1) * BANK // 16]
+            nc.vector.tensor_copy(both[:].bitcast(U32), tab_w[:].bitcast(U32).indirect(listed))
+            parted = sb("tab_parted%d" % h, [P, PASSES * 2 * BANK], U8)
+            nc.vector.tensor_copy(
+                out=parted[:].bitcast(U16).rearrange("p (a j) -> p a j", a=PASSES),
+                in_=both[:].bitcast(U16).rearrange("p (j a) -> p a j", a=PASSES),
+            )
             for a in range(PASSES):
-                tab_codes[a, h] = parted[a][:].bitcast(FP4X4)
+                tab_codes[a, h] = parted[:, a * 2 * BANK : (a + 1) * 2 * BANK].bitcast(FP4X4)
 
         def with_table(out, codes, scales, a, h, start, stop):
             nc.tensor.matmul_mx(
@@ -179,30 +172,29 @@ def tile_list_mlat_outl_dl_exp_kernel(
                 stop=stop,
             )
 
+        wvd_bf = {}
         wvd_q = {}
+        x_bf = {}
+        x_q = {}
+        vv_bank = {}
 
-        def prepare_wvd(a, g):
-            grouped = interleave("wvd_bf%d%d" % (a, g), wvd_raw[a][:, :, g * UNIT : (g + 1) * UNIT], True)
-            wvd_q[a, g] = quantize("wvd%d%d" % (a, g), grouped[:], UNIT)
+        def cast_wvd(a, g, on_scalar):
+            wvd_bf[a, g] = interleave("wvd_bf%d%d" % (a, g), wvd_raw[a, g][:], on_scalar)
 
-        early = [(nt, h) for nt in range(N // P) for h in range(2)][:EARLY]
-        vv_bank = {key: next_bank() for key in early}
+        def quantize_wvd(a, g):
+            wvd_q[a, g] = quantize("wvd%d%d" % (a, g), wvd_bf[a, g], UNIT)
+
+        def cast_x(a, u, on_scalar):
+            x_bf[a, u] = interleave("x_bf%d_%d" % (a, u), x_raw[a, u], on_scalar)
+
+        def quantize_x(a, u):
+            codes, scales = quantize("x%d_%d" % (a, u), x_bf[a, u], UNIT)
+            for n in range(2):
+                x_q[a, 2 * u + n] = codes[:, P * n : P * (n + 1)].bitcast(FP8X4), scales[:, P * n : P * (n + 1)]
 
         def vv_base(a, nt, h):
             codes = wv4_w[:, a, 2 * P * nt : 2 * P * (nt + 1)].bitcast(FP4X4)
             with_table(vv_bank[nt, h][:], codes, wv4_sc[:, a, P * nt : P * (nt + 1)], a, h, a == 0, False)
-
-        def warm_up(passes):
-            for n in range(passes):
-                nc.tensor.matmul_mx(
-                    out=banks[7][:],
-                    lhsT=wv4_w[:, 0, 0 : 2 * P].bitcast(FP4X4),
-                    lhsT_scale=plane0[:, 0:P],
-                    rhs=wv4_w[:, 0, :].bitcast(FP4X4),
-                    rhs_scale=plane0[:, 0:BANK],
-                    start=True,
-                    stop=True,
-                )
 
         def vv_delta(a, nt, h):
             codes, scales = wvd_q[a, nt // 2]
@@ -219,10 +211,6 @@ def tile_list_mlat_outl_dl_exp_kernel(
             w8_p = sb("w8_p", [P, R], I32)
             w4_p = sb("w4_p", [P, 2 * R], U8)
             w_sc = sb("w_sc", [P, R], U8)
-            nc.vector.tensor_copy(
-                out=w_sc[:].rearrange("p (a i m) -> p a i m", a=PASSES, i=PACK),
-                in_=w_sc_raw[:].rearrange("p (a m i) -> p a i m", a=PASSES, i=PACK),
-            )
             for a in range(PASSES):
                 cols = slice(a * K_PASS, (a + 1) * K_PASS)
                 nc.vector.tensor_copy(
@@ -233,103 +221,127 @@ def tile_list_mlat_outl_dl_exp_kernel(
                 out=w4_p[:].bitcast(U16).rearrange("p (a i m) -> p a i m", a=PASSES, i=PACK),
                 in_=w4_raw[:].bitcast(U16).rearrange("p (a m i) -> p a i m", a=PASSES, i=PACK),
             )
+            nc.vector.tensor_copy(
+                out=w_sc[:].rearrange("p (a i m) -> p a i m", a=PASSES, i=PACK),
+                in_=w_sc_raw[:].rearrange("p (a m i) -> p a i m", a=PASSES, i=PACK),
+            )
             return w8_p, w4_p, w_sc
-
-        x_q = {}
-
-        def prepare_x(a, mt, count, on_scalar):
-            raw = x_raw[a, mt // 2][:, :, P * (mt % 2) : P * (mt % 2 + count)]
-            grouped = interleave("x_bf%d_%d" % (a, mt), raw, on_scalar)
-            codes, scales = quantize("x%d_%d" % (a, mt), grouped[:], P * count)
-            for n in range(count):
-                x_q[a, mt + n] = codes[:, P * n : P * (n + 1)].bitcast(FP8X4), scales[:, P * n : P * (n + 1)]
 
         qa_q = {}
 
-        def project(mt, engines):
+        def project(mt, pair, orders):
             grouped = []
+            for a, kp in orders:
+                for i in range(PACK):
+                    c = a * K_PASS + i * P
+                    if kp == 0:
+                        w_codes, w_plane = w8_p[:, c : c + P].bitcast(FP8X4), w_sc[ROWS:P, c : c + P]
+                    else:
+                        w_codes, w_plane = w4_p[:, 2 * c : 2 * (c + P)].bitcast(FP4X4), w_sc[:, c : c + P]
+                    x_codes, x_plane = x_q[kp, mt]
+                    first = (a, 1 - kp) not in orders[: orders.index((a, kp))]
+                    nc.tensor.matmul_mx(
+                        out=pair[a][:, i * P : (i + 1) * P],
+                        lhsT=w_codes,
+                        lhsT_scale=w_plane,
+                        rhs=x_codes,
+                        rhs_scale=x_plane,
+                        start=(first and i == 0),
+                        stop=(not first and i == PACK - 1),
+                    )
             for a in range(PASSES):
-                bank = next_bank()
-                order = (0, 1) if a == 0 else (1, 0)
-                for kp in order:
-                    for i in range(PACK):
-                        c = a * K_PASS + i * P
-                        if kp == 0:
-                            w_codes, w_plane = w8_p[:, c : c + P].bitcast(FP8X4), w_sc[ROWS:P, c : c + P]
-                        else:
-                            w_codes, w_plane = w4_p[:, 2 * c : 2 * (c + P)].bitcast(FP4X4), w_sc[:, c : c + P]
-                        x_codes, x_plane = x_q[kp, mt]
-                        nc.tensor.matmul_mx(
-                            out=bank[:, i * P : (i + 1) * P],
-                            lhsT=w_codes,
-                            lhsT_scale=w_plane,
-                            rhs=x_codes,
-                            rhs_scale=x_plane,
-                            start=(kp == order[0] and i == 0),
-                            stop=(kp == order[1] and i == PACK - 1),
-                        )
                 qa_bf = sb("qa_bf%d_%d" % (a, mt), [P, K_PASS], BF16)
-                copy_on(engines[a], qa_bf[:].rearrange("p (m i) -> p m i", i=PACK), bank[:].rearrange("p (i m) -> p m i", i=PACK))
+                copy_on(a == 0, qa_bf[:].rearrange("p (m i) -> p m i", i=PACK), pair[a][:].rearrange("p (i m) -> p m i", i=PACK))
                 grouped.append(qa_bf)
             for a in range(PASSES):
-                qa_q[a, mt] = quantize("qa%d_%d" % (a, mt), grouped[a][:], P)
+                qa_q[a, mt] = quantize("qa%d_%d" % (a, mt), grouped[a], P)
 
-        def score(mt, split_store, pieces=((0, BANK), (BANK, J))):
-            pair = [next_bank(), next_bank()]
+        def score(mt, pair, split_store):
             order = [(a, h) for h in range(2) for a in range(PASSES)] if split_store else [(a, h) for a in range(PASSES) for h in range(2)]
             for a, h in order:
                 codes, scales = qa_q[a, mt]
                 with_table(pair[h][:], codes[:].bitcast(FP8X4), scales[:], a, h, a == 0, a == PASSES - 1)
             res = sb("sc_res%d" % mt, [P, J], F32)
             rows = slice(P * mt, P * (mt + 1))
-            for c0, c1 in pieces:
-                h = c0 // BANK
-                nc.scalar.activation(
-                    out=res[:, c0:c1], in_=pair[h][:, c0 - h * BANK : c1 - h * BANK], func=EXP, bias=no_bias[:], scale=SCORE_SCALE
-                )
+            for h in range(2):
+                cols = slice(h * BANK, (h + 1) * BANK)
+                nc.scalar.activation(out=res[:, cols], in_=pair[h][:], func=EXP, bias=no_bias[:], scale=SCORE_SCALE)
                 if split_store:
-                    nc.sync.dma_start(out=out_0[rows, c0:c1], in_=res[:, c0:c1])
+                    nc.sync.dma_start(out=out_0[rows, cols], in_=res[:, cols])
             if not split_store:
                 nc.sync.dma_start(out=out_0[rows, :], in_=res[:])
 
-        gather_scales()
-        move_scales()
-        for h in range(2):
-            gather_words(h)
-            for nt, hh in early:
-                if hh == h:
-                    vv_base(0, nt, h)
-        for g in range(2):
-            prepare_wvd(0, g)
-        for nt, h in early:
-            vv_delta(0, nt, h)
-        w8_p, w4_p, w_sc = permute_w()
-        for g in range(2):
-            prepare_wvd(1, g)
+        W8_FIRST = [(0, 0), (1, 0), (0, 1), (1, 1)]
+        BY_BANK = [(0, 0), (0, 1), (1, 1), (1, 0)]
+
         for nt in range(4):
-            for step in (vv_base, vv_delta):
-                for h in range(2):
-                    if (nt, h) in early:
-                        step(1, nt, h)
-        prepare_x(0, 0, 2, False)
-        prepare_x(1, 0, 1, False)
-        prepare_x(1, 1, 1, False)
-        prepare_x(0, 2, 2, False)
+            vv_bank[nt, 0] = banks[nt]
+        for nt in range(2):
+            vv_bank[nt, 1] = banks[4 + nt]
+        gather_words(0)
+        for nt in range(4):
+            vv_base(0, nt, 0)
+        gather_words(1)
+        for nt in range(2):
+            vv_base(0, nt, 1)
+        cast_wvd(0, 0, True)
+        quantize_wvd(0, 0)
+        for nt in range(2):
+            for h in range(2):
+                vv_delta(0, nt, h)
+        for nt, h in vv_bank:
+            vv_base(1, nt, h)
+        cast_wvd(1, 0, True)
+        quantize_wvd(1, 0)
+        for nt in range(2):
+            for h in range(2):
+                vv_delta(1, nt, h)
+        w8_p, w4_p, w_sc = permute_w()
+        for a in range(PASSES):
+            cast_x(a, 0, False)
+            quantize_x(a, 0)
         vv_store(0, (0, 1), True)
         vv_store(1, (0, 1), True)
-        tiles = M // P
-        project(0, (True, False))
-        vv_store(2, (0, 1), True)
+        for a in range(PASSES):
+            cast_wvd(a, 1, False)
+        for a in range(PASSES):
+            quantize_wvd(a, 1)
+        project(0, (banks[6], banks[7]), W8_FIRST)
+        project(1, (banks[0], banks[4]), BY_BANK)
+        for a in range(PASSES):
+            for nt in range(2, 4):
+                vv_delta(a, nt, 0)
+        for a in range(PASSES):
+            cast_x(a, 1, False)
+        for a in range(PASSES):
+            quantize_x(a, 1)
+        score(0, (banks[1], banks[5]), False)
+        vv_store(2, (0,), True)
         vv_store(3, (0,), True)
-        for mt in range(1, tiles):
-            a, u = mt % 2, (mt + 2) // 2
-            if u < M // UNIT:
-                prepare_x(a, 2 * u, 2, mt in (1,2,3,4,5))
-            project(mt, (mt in (6, 7), False))
-            score(mt - 1, mt - 1 >= tiles - 2)
-        vv_bank[3, 1] = next_bank()
-        for step in (vv_base, vv_delta):
-            for a in range(PASSES):
-                step(a, 3, 1)
-        vv_store(3, (1,), False)
-        score(tiles - 1, True)
+
+        ring = [banks[b] for b in (6, 7, 0, 4, 2, 3, 1, 5)]
+        taken = []
+
+        def next_bank():
+            taken.append(ring[len(taken) % len(ring)])
+            return taken[-1]
+
+        def vv_whole(nt):
+            vv_bank[nt, 1] = next_bank()
+            for step in (vv_base, vv_delta):
+                for a in range(PASSES):
+                    step(a, nt, 1)
+            vv_store(nt, (1,), False)
+
+        tiles = M // P
+        for mt in range(2, tiles):
+            if mt < tiles - 2:
+                a, u = mt % 2, mt // 2 + 1
+                cast_x(a, u, False)
+                quantize_x(a, u)
+            project(mt, (next_bank(), next_bank()), BY_BANK)
+            score(mt - 1, (next_bank(), next_bank()), mt - 1 >= tiles - 2)
+            if mt == 2:
+                vv_whole(2)
+        vv_whole(3)
+        score(tiles - 1, (next_bank(), next_bank()), True)

@@ -65,7 +65,7 @@ def tile_list_mlat_outl_dl_exp_kernel(
         nc.vector.memset(zero[:], 0.0)
 
         def load_rows(name, src, a, c0, width):
-            raw = sb(name, [P, PACK, width], F32)
+            raw = sb(name, [P, PACK, width], F32, name)
             rows = src[a * K_PASS : (a + 1) * K_PASS, c0 : c0 + width]
             nc.sync.dma_start(out=raw[:], in_=rows.rearrange("(p i) c -> p i c", i=PACK))
             return raw
@@ -85,8 +85,8 @@ def tile_list_mlat_outl_dl_exp_kernel(
         wvd_raw = {}
         x_raw = {}
 
-        def load_wvd(a, g):
-            wvd_raw[a, g] = load_rows("wvd_raw%d_%d" % (a, g), wvd, a, g * UNIT, UNIT)
+        def load_wvd(a):
+            wvd_raw[a] = load_rows("wvd_raw%d" % a, wvd, a, 0, N)
 
         def load_x(a, u0, count):
             raw = load_rows("x_raw%d_%d" % (a, u0), x, a, u0 * UNIT, count * UNIT)
@@ -95,7 +95,6 @@ def tile_list_mlat_outl_dl_exp_kernel(
 
         plane0 = sb("plane0", [P, J], U8)
         tab_planes = [plane0, plane1]
-        tab_codes = {}
         nc.sync.dma_start(offsets[:], offs)
         for q in range(4):
             (nc.sync if q < 2 else nc.scalar).dma_start(
@@ -109,27 +108,26 @@ def tile_list_mlat_outl_dl_exp_kernel(
         nc.sync.dma_start(out=tab_w[:], in_=tab_words[0].rearrange("p t b -> p (t b)").bitcast(I32))
         load_wv4_scales(nc.sync, 2)
         load_wv4_scales(nc.sync, 3)
-        for q in range(2):
-            load_w_scales(w8_scales, ROWS, q)
+        load_w_scales(w8_scales, ROWS, 0)
         nc.sync.dma_start(out=wv4_w[:].bitcast(I32), in_=wv4_words.rearrange("a p c -> p a c").bitcast(I32))
-        load_wvd(0, 0)
-        load_wvd(1, 0)
+        load_wvd(0)
+        load_w_scales(w8_scales, ROWS, 1)
+        nc.sync.dma_start(out=w4_raw[:].bitcast(I32), in_=w4_words[0].bitcast(I32))
         nc.vector.tensor_copy(plane0[:], tab_sc[:].indirect(offsets[:]))
         for q in range(4):
             nc.sync.dma_start(
                 out=plane1[32 * q : 32 * q + ROWS, :].bitcast(I32),
                 in_=plane0[32 * q + ROWS : 32 * q + 2 * ROWS, :].bitcast(I32),
             )
-        nc.sync.dma_start(out=w8_raw[:], in_=w8_words[0].rearrange("p r b -> p (r b)").bitcast(I32))
-        nc.sync.dma_start(out=w4_raw[:].bitcast(I32), in_=w4_words[0].bitcast(I32))
+        load_wvd(1)
         load_w_scales(w8_scales, ROWS, 2)
-        load_x(0, 0, 1)
+        nc.sync.dma_start(out=w8_raw[:], in_=w8_words[0].rearrange("p r b -> p (r b)").bitcast(I32))
         load_w_scales(w8_scales, ROWS, 3)
-        for q in range(4):
+        for q in range(3):
             load_w_scales(w4_scales, 0, q)
+        load_x(0, 0, 1)
+        load_w_scales(w4_scales, 0, 3)
         load_x(1, 0, 1)
-        load_wvd(0, 1)
-        load_wvd(1, 1)
         for u0, count in ((1, 1), (2, 2)):
             for a in range(PASSES):
                 load_x(a, u0, count)
@@ -149,25 +147,26 @@ def tile_list_mlat_outl_dl_exp_kernel(
             nc.vector.quantize_mx(out=codes[:].bitcast(FP8X4), scales=scales[:], in_=grouped[:])
             return codes, scales
 
-        def gather_words(h):
-            both = sb("tab_both%d" % h, [P, BANK], I32, "tab_both")
-            listed = offsets[:, h * BANK // 16 : (h + 1) * BANK // 16]
+        parted = [sb("tab_parted%d" % h, [P, PASSES * 2 * BANK], U8) for h in range(2)]
+
+        def gather_words(j0, count):
+            both = sb("tab_both%d" % j0, [P, count], I32, "tab_both")
+            listed = offsets[:, j0 // 16 : (j0 + count) // 16]
             nc.vector.tensor_copy(both[:].bitcast(U32), tab_w[:].bitcast(U32).indirect(listed))
-            parted = sb("tab_parted%d" % h, [P, PASSES * 2 * BANK], U8)
+            c0 = j0 % BANK
             nc.vector.tensor_copy(
-                out=parted[:].bitcast(U16).rearrange("p (a j) -> p a j", a=PASSES),
+                out=parted[j0 // BANK][:].bitcast(U16).rearrange("p (a j) -> p a j", a=PASSES)[:, :, c0 : c0 + count],
                 in_=both[:].bitcast(U16).rearrange("p (j a) -> p a j", a=PASSES),
             )
-            for a in range(PASSES):
-                tab_codes[a, h] = parted[:, a * 2 * BANK : (a + 1) * 2 * BANK].bitcast(FP4X4)
 
-        def with_table(out, codes, scales, a, h, start, stop):
+        def with_table(out, codes, scales, a, j0, count, start, stop):
+            c0 = a * BANK + j0 % BANK
             nc.tensor.matmul_mx(
                 out=out,
                 lhsT=codes,
                 lhsT_scale=scales,
-                rhs=tab_codes[a, h],
-                rhs_scale=tab_planes[a][:, h * BANK : (h + 1) * BANK],
+                rhs=parted[j0 // BANK][:, 2 * c0 : 2 * (c0 + count)].bitcast(FP4X4),
+                rhs_scale=tab_planes[a][:, j0 : j0 + count],
                 start=start,
                 stop=stop,
             )
@@ -179,7 +178,7 @@ def tile_list_mlat_outl_dl_exp_kernel(
         vv_bank = {}
 
         def cast_wvd(a, g, on_scalar):
-            wvd_bf[a, g] = interleave("wvd_bf%d%d" % (a, g), wvd_raw[a, g][:], on_scalar)
+            wvd_bf[a, g] = interleave("wvd_bf%d%d" % (a, g), wvd_raw[a][:, :, g * UNIT : (g + 1) * UNIT], on_scalar)
 
         def quantize_wvd(a, g):
             wvd_q[a, g] = quantize("wvd%d%d" % (a, g), wvd_bf[a, g], UNIT)
@@ -192,20 +191,21 @@ def tile_list_mlat_outl_dl_exp_kernel(
             for n in range(2):
                 x_q[a, 2 * u + n] = codes[:, P * n : P * (n + 1)].bitcast(FP8X4), scales[:, P * n : P * (n + 1)]
 
-        def vv_base(a, nt, h):
+        def vv_base(out, a, nt, j0, count, start):
             codes = wv4_w[:, a, 2 * P * nt : 2 * P * (nt + 1)].bitcast(FP4X4)
-            with_table(vv_bank[nt, h][:], codes, wv4_sc[:, a, P * nt : P * (nt + 1)], a, h, a == 0, False)
+            with_table(out, codes, wv4_sc[:, a, P * nt : P * (nt + 1)], a, j0, count, start, False)
 
-        def vv_delta(a, nt, h):
+        def vv_delta(out, a, nt, j0, count, stop):
             codes, scales = wvd_q[a, nt // 2]
             cols = slice(P * (nt % 2), P * (nt % 2 + 1))
-            with_table(vv_bank[nt, h][:], codes[:, cols].bitcast(FP8X4), scales[:, cols], a, h, False, a == PASSES - 1)
+            with_table(out, codes[:, cols].bitcast(FP8X4), scales[:, cols], a, j0, count, False, stop)
 
-        def vv_store(nt, halves, on_scalar):
-            res = sb("vv_res%d_%d" % (nt, halves[0]), [P, BANK * len(halves)], F32)
-            for n, h in enumerate(halves):
-                copy_on(on_scalar, res[:, n * BANK : (n + 1) * BANK], vv_bank[nt, h][:])
-            nc.sync.dma_start(out=out_1[P * nt : P * (nt + 1), halves[0] * BANK : (halves[-1] + 1) * BANK], in_=res[:])
+        def vv_store(res, nt, j0, parts, on_scalar):
+            c0 = 0
+            for part in parts:
+                copy_on(on_scalar, res[:, c0 : c0 + part.shape[1]], part)
+                c0 += part.shape[1]
+            nc.sync.dma_start(out=out_1[P * nt : P * (nt + 1), j0 : j0 + c0], in_=res)
 
         def permute_w():
             w8_p = sb("w8_p", [P, R], I32)
@@ -260,7 +260,7 @@ def tile_list_mlat_outl_dl_exp_kernel(
             order = [(a, h) for h in range(2) for a in range(PASSES)] if split_store else [(a, h) for a in range(PASSES) for h in range(2)]
             for a, h in order:
                 codes, scales = qa_q[a, mt]
-                with_table(pair[h][:], codes[:].bitcast(FP8X4), scales[:], a, h, a == 0, a == PASSES - 1)
+                with_table(pair[h][:], codes[:].bitcast(FP8X4), scales[:], a, h * BANK, BANK, a == 0, a == PASSES - 1)
             res = sb("sc_res%d" % mt, [P, J], F32)
             rows = slice(P * mt, P * (mt + 1))
             for h in range(2):
@@ -274,64 +274,56 @@ def tile_list_mlat_outl_dl_exp_kernel(
         W8_FIRST = [(0, 0), (1, 0), (0, 1), (1, 1)]
         BY_BANK = [(0, 0), (0, 1), (1, 1), (1, 0)]
 
-        for nt in range(4):
-            vv_bank[nt, 0] = banks[nt]
-        for nt in range(2):
-            vv_bank[nt, 1] = banks[4 + nt]
-        gather_words(0)
-        for nt in range(4):
-            vv_base(0, nt, 0)
-        gather_words(1)
-        for nt in range(2):
-            vv_base(0, nt, 1)
-        cast_wvd(0, 0, True)
-        quantize_wvd(0, 0)
-        for nt in range(2):
-            for h in range(2):
-                vv_delta(0, nt, h)
-        for nt, h in vv_bank:
-            vv_base(1, nt, h)
-        cast_wvd(1, 0, True)
-        quantize_wvd(1, 0)
-        for nt in range(2):
-            for h in range(2):
-                vv_delta(1, nt, h)
+        early = [(0, 0), (1, 0), (2, 0), (3, 0), (0, 1), (1, 1), (2, 1)]
+        for n, key in enumerate(early):
+            vv_bank[key] = banks[n]
+
+        def base(a, keys, start):
+            for nt, h in keys:
+                vv_base(vv_bank[nt, h][:], a, nt, h * BANK, BANK, start)
+
+        def delta(a, keys):
+            for nt, h in keys:
+                vv_delta(vv_bank[nt, h][:], a, nt, h * BANK, BANK, a == PASSES - 1)
+
+        for j0 in (0, UNIT):
+            gather_words(j0, UNIT)
+            for nt in range(4):
+                vv_base(vv_bank[nt, 0][:, j0 : j0 + UNIT], 0, nt, j0, UNIT, j0 == 0)
+        gather_words(BANK, BANK)
+        base(1, early[:4], False)
+        base(1, early[4:], True)
+        base(0, early[4:], False)
+        for a in range(PASSES):
+            for g, keys in enumerate(([(0, 0), (0, 1), (1, 0), (1, 1)], [(2, 0), (2, 1), (3, 0)])):
+                cast_wvd(a, g, True)
+                quantize_wvd(a, g)
+                delta(a, keys)
         w8_p, w4_p, w_sc = permute_w()
         for a in range(PASSES):
-            cast_x(a, 0, False)
+            cast_x(a, 0, a == 1)
             quantize_x(a, 0)
-        vv_store(0, (0, 1), True)
-        vv_store(1, (0, 1), True)
-        for a in range(PASSES):
-            cast_wvd(a, 1, False)
-        for a in range(PASSES):
-            quantize_wvd(a, 1)
-        project(0, (banks[6], banks[7]), W8_FIRST)
-        project(1, (banks[0], banks[4]), BY_BANK)
-        for a in range(PASSES):
-            for nt in range(2, 4):
-                vv_delta(a, nt, 0)
+        vv_res = sb("vv_res", [P, 3 * J], F32, "x_raw1_0")
+        for nt in range(2):
+            vv_store(vv_res[:, nt * J : (nt + 1) * J], nt, 0, [vv_bank[nt, h][:] for h in range(2)], True)
         for a in range(PASSES):
             cast_x(a, 1, False)
         for a in range(PASSES):
             quantize_x(a, 1)
-        score(0, (banks[1], banks[5]), False)
-        vv_store(2, (0,), True)
-        vv_store(3, (0,), True)
+        project(0, (banks[7], vv_bank[0, 0]), W8_FIRST)
+        copy_on(True, vv_res[:, 2 * J : 2 * J + BANK], vv_bank[2, 0][:])
+        project(1, (vv_bank[0, 1], vv_bank[1, 0]), BY_BANK)
+        copy_on(True, vv_res[:, 2 * J + BANK :], vv_bank[2, 1][:])
+        nc.sync.dma_start(out=out_1[2 * P : 3 * P, :], in_=vv_res[:, 2 * J :])
+        vv_store(sb("vv_res3", [P, BANK], F32, "x_bf1_0")[:], 3, 0, [vv_bank[3, 0][:]], False)
+        score(0, (vv_bank[1, 1], vv_bank[2, 0]), False)
 
-        ring = [banks[b] for b in (6, 7, 0, 4, 2, 3, 1, 5)]
+        ring = [banks[b] for b in (3, 6, 7, 0, 4, 1, 5, 2)]
         taken = []
 
-        def next_bank():
-            taken.append(ring[len(taken) % len(ring)])
-            return taken[-1]
-
-        def vv_whole(nt):
-            vv_bank[nt, 1] = next_bank()
-            for step in (vv_base, vv_delta):
-                for a in range(PASSES):
-                    step(a, nt, 1)
-            vv_store(nt, (1,), False)
+        def next_pair():
+            taken.append(len(taken))
+            return ring[2 * taken[-1] % 8], ring[(2 * taken[-1] + 1) % 8]
 
         tiles = M // P
         for mt in range(2, tiles):
@@ -339,9 +331,16 @@ def tile_list_mlat_outl_dl_exp_kernel(
                 a, u = mt % 2, mt // 2 + 1
                 cast_x(a, u, False)
                 quantize_x(a, u)
-            project(mt, (next_bank(), next_bank()), BY_BANK)
-            score(mt - 1, (next_bank(), next_bank()), mt - 1 >= tiles - 2)
-            if mt == 2:
-                vv_whole(2)
-        vv_whole(3)
-        score(tiles - 1, (next_bank(), next_bank()), True)
+            project(mt, next_pair(), BY_BANK)
+            if mt < tiles - 2:
+                score(mt - 1, next_pair(), False)
+        for mt in range(tiles - 3, tiles):
+            score(mt, next_pair(), True)
+        for n, bank in enumerate(next_pair()):
+            j0 = BANK + n * UNIT
+            for a in range(PASSES):
+                vv_base(bank[:, :UNIT], a, 3, j0, UNIT, a == 0)
+            for a in range(PASSES):
+                for c0 in (0, P):
+                    vv_delta(bank[:, c0 : c0 + P], a, 3, j0 + c0, P, a == PASSES - 1 and c0 == P)
+            vv_store(sb("vv_last%d" % n, [P, UNIT], F32)[:], 3, j0, [bank[:, :UNIT]], n == 1)

@@ -70,8 +70,8 @@ def tile_list_mlat_outl_dl_exp_kernel(
             nc.sync.dma_start(out=raw[:], in_=rows.rearrange("(p i) c -> p i c", i=PACK))
             return raw
 
-        def load_wv4_scales(queue, q):
-            queue.dma_start(
+        def load_wv4_scales(q):
+            nc.sync.dma_start(
                 out=wv4_sc[32 * q : 32 * q + ROWS].bitcast(I32),
                 in_=wv4_scales[:, ROWS * q : ROWS * (q + 1), :].rearrange("a r c -> r a c").bitcast(I32),
             )
@@ -96,22 +96,22 @@ def tile_list_mlat_outl_dl_exp_kernel(
         plane0 = sb("plane0", [P, J], U8)
         tab_planes = [plane0, plane1]
         nc.sync.dma_start(offsets[:], offs)
+        nc.sync.dma_start(out=wv4_w[:].bitcast(I32), in_=wv4_words.rearrange("a p c -> p a c").bitcast(I32))
         for q in range(4):
             (nc.sync if q < 2 else nc.scalar).dma_start(
                 out=tab_sc[32 * q : 32 * q + PASSES * ROWS, :].bitcast(I32),
                 in_=tab_scales[:, ROWS * q : ROWS * (q + 1), :].bitcast(I32),
             )
-        load_wv4_scales(nc.scalar, 0)
-        load_wv4_scales(nc.scalar, 1)
+        load_wv4_scales(0)
         no_bias = sb("no_bias", [P, 1], F32)
         nc.scalar.activation(out=no_bias[:], in_=zero[:], func=COPY)
         nc.sync.dma_start(out=tab_w[:], in_=tab_words[0].rearrange("p t b -> p (t b)").bitcast(I32))
-        load_wv4_scales(nc.sync, 2)
-        load_wv4_scales(nc.sync, 3)
-        load_w_scales(w8_scales, ROWS, 0)
-        nc.sync.dma_start(out=wv4_w[:].bitcast(I32), in_=wv4_words.rearrange("a p c -> p a c").bitcast(I32))
+        for q in range(1, 4):
+            load_wv4_scales(q)
+        for q in range(2):
+            load_w_scales(w8_scales, ROWS, q)
         load_wvd(0)
-        load_w_scales(w8_scales, ROWS, 1)
+        load_w_scales(w8_scales, ROWS, 2)
         nc.sync.dma_start(out=w4_raw[:].bitcast(I32), in_=w4_words[0].bitcast(I32))
         nc.vector.tensor_copy(plane0[:], tab_sc[:].indirect(offsets[:]))
         for q in range(4):
@@ -120,20 +120,15 @@ def tile_list_mlat_outl_dl_exp_kernel(
                 in_=plane0[32 * q + ROWS : 32 * q + 2 * ROWS, :].bitcast(I32),
             )
         load_wvd(1)
-        load_w_scales(w8_scales, ROWS, 2)
         nc.sync.dma_start(out=w8_raw[:], in_=w8_words[0].rearrange("p r b -> p (r b)").bitcast(I32))
         load_w_scales(w8_scales, ROWS, 3)
-        for q in range(3):
+        for q in range(4):
             load_w_scales(w4_scales, 0, q)
-        load_x(0, 0, 1)
-        load_w_scales(w4_scales, 0, 3)
-        load_x(1, 0, 1)
-        for u0, count in ((1, 1), (2, 2)):
-            for a in range(PASSES):
-                load_x(a, u0, count)
+        for a, u0, count in ((0, 0, 2), (1, 0, 1), (1, 1, 1), (0, 2, 2), (1, 2, 1), (1, 3, 1)):
+            load_x(a, u0, count)
 
         def interleave(name, raw, on_scalar):
-            grouped = sb(name, [P, UNIT * PACK], BF16)
+            grouped = sb(name, [P, raw.shape[2] * PACK], BF16)
             copy_on(
                 on_scalar,
                 grouped[:].rearrange("p (c j i) -> p c i j", j=4, i=PACK),
@@ -141,8 +136,8 @@ def tile_list_mlat_outl_dl_exp_kernel(
             )
             return grouped
 
-        def quantize(name, grouped, cols):
-            codes = sb(name + "_codes", [P, cols], U32)
+        def quantize(name, grouped, cols, slot=None):
+            codes = sb(name + "_codes", [P, cols], U32, slot)
             scales = sb(name + "_scales", [P, cols], U8)
             nc.vector.quantize_mx(out=codes[:].bitcast(FP8X4), scales=scales[:], in_=grouped[:])
             return codes, scales
@@ -150,7 +145,7 @@ def tile_list_mlat_outl_dl_exp_kernel(
         parted = [sb("tab_parted%d" % h, [P, PASSES * 2 * BANK], U8) for h in range(2)]
 
         def gather_words(j0, count):
-            both = sb("tab_both%d" % j0, [P, count], I32, "tab_both")
+            both = sb("tab_both%d" % j0, [P, count], I32, "tab_both%d" % (j0 // count % 2))
             listed = offsets[:, j0 // 16 : (j0 + count) // 16]
             nc.vector.tensor_copy(both[:].bitcast(U32), tab_w[:].bitcast(U32).indirect(listed))
             c0 = j0 % BANK
@@ -180,16 +175,17 @@ def tile_list_mlat_outl_dl_exp_kernel(
         def cast_wvd(a, g, on_scalar):
             wvd_bf[a, g] = interleave("wvd_bf%d%d" % (a, g), wvd_raw[a][:, :, g * UNIT : (g + 1) * UNIT], on_scalar)
 
-        def quantize_wvd(a, g):
-            wvd_q[a, g] = quantize("wvd%d%d" % (a, g), wvd_bf[a, g], UNIT)
+        def quantize_wvd(a, g, slot=None):
+            wvd_q[a, g] = quantize("wvd%d%d" % (a, g), wvd_bf[a, g], UNIT, slot)
 
-        def cast_x(a, u, on_scalar):
-            x_bf[a, u] = interleave("x_bf%d_%d" % (a, u), x_raw[a, u], on_scalar)
+        def cast_x(a, mt, count, on_scalar):
+            c0 = P * (mt % 2)
+            x_bf[a, mt] = interleave("x_bf%d_%d" % (a, mt), x_raw[a, mt // 2][:, :, c0 : c0 + count * P], on_scalar)
 
-        def quantize_x(a, u):
-            codes, scales = quantize("x%d_%d" % (a, u), x_bf[a, u], UNIT)
-            for n in range(2):
-                x_q[a, 2 * u + n] = codes[:, P * n : P * (n + 1)].bitcast(FP8X4), scales[:, P * n : P * (n + 1)]
+        def quantize_x(a, mt, count):
+            codes, scales = quantize("x%d_%d" % (a, mt), x_bf[a, mt], count * P)
+            for n in range(count):
+                x_q[a, mt + n] = codes[:, P * n : P * (n + 1)].bitcast(FP8X4), scales[:, P * n : P * (n + 1)]
 
         def vv_base(out, a, nt, j0, count, start):
             codes = wv4_w[:, a, 2 * P * nt : 2 * P * (nt + 1)].bitcast(FP4X4)
@@ -229,32 +225,37 @@ def tile_list_mlat_outl_dl_exp_kernel(
 
         qa_q = {}
 
-        def project(mt, pair, orders):
+        def project_passes(mt, bank, a, kp, first):
+            for i in range(PACK):
+                c = a * K_PASS + i * P
+                if kp == 0:
+                    w_codes, w_plane = w8_p[:, c : c + P].bitcast(FP8X4), w_sc[ROWS:P, c : c + P]
+                else:
+                    w_codes, w_plane = w4_p[:, 2 * c : 2 * (c + P)].bitcast(FP4X4), w_sc[:, c : c + P]
+                x_codes, x_plane = x_q[kp, mt]
+                nc.tensor.matmul_mx(
+                    out=bank[:, i * P : (i + 1) * P],
+                    lhsT=w_codes,
+                    lhsT_scale=w_plane,
+                    rhs=x_codes,
+                    rhs_scale=x_plane,
+                    start=(first and i == 0),
+                    stop=(not first and i == PACK - 1),
+                )
+
+        def quantize_qa(mt, pair, both_on_scalar):
             grouped = []
-            for a, kp in orders:
-                for i in range(PACK):
-                    c = a * K_PASS + i * P
-                    if kp == 0:
-                        w_codes, w_plane = w8_p[:, c : c + P].bitcast(FP8X4), w_sc[ROWS:P, c : c + P]
-                    else:
-                        w_codes, w_plane = w4_p[:, 2 * c : 2 * (c + P)].bitcast(FP4X4), w_sc[:, c : c + P]
-                    x_codes, x_plane = x_q[kp, mt]
-                    first = (a, 1 - kp) not in orders[: orders.index((a, kp))]
-                    nc.tensor.matmul_mx(
-                        out=pair[a][:, i * P : (i + 1) * P],
-                        lhsT=w_codes,
-                        lhsT_scale=w_plane,
-                        rhs=x_codes,
-                        rhs_scale=x_plane,
-                        start=(first and i == 0),
-                        stop=(not first and i == PACK - 1),
-                    )
             for a in range(PASSES):
                 qa_bf = sb("qa_bf%d_%d" % (a, mt), [P, K_PASS], BF16)
-                copy_on(a == 0, qa_bf[:].rearrange("p (m i) -> p m i", i=PACK), pair[a][:].rearrange("p (i m) -> p m i", i=PACK))
+                copy_on(a == 0 or both_on_scalar, qa_bf[:].rearrange("p (m i) -> p m i", i=PACK), pair[a][:].rearrange("p (i m) -> p m i", i=PACK))
                 grouped.append(qa_bf)
             for a in range(PASSES):
                 qa_q[a, mt] = quantize("qa%d_%d" % (a, mt), grouped[a], P)
+
+        def project(mt, pair):
+            for a, kp, first in ((0, 0, True), (0, 1, False), (1, 1, True), (1, 0, False)):
+                project_passes(mt, pair[a], a, kp, first)
+            quantize_qa(mt, pair, False)
 
         def score(mt, pair, split_store):
             order = [(a, h) for h in range(2) for a in range(PASSES)] if split_store else [(a, h) for a in range(PASSES) for h in range(2)]
@@ -270,9 +271,6 @@ def tile_list_mlat_outl_dl_exp_kernel(
                     nc.sync.dma_start(out=out_0[rows, cols], in_=res[:, cols])
             if not split_store:
                 nc.sync.dma_start(out=out_0[rows, :], in_=res[:])
-
-        W8_FIRST = [(0, 0), (1, 0), (0, 1), (1, 1)]
-        BY_BANK = [(0, 0), (0, 1), (1, 1), (1, 0)]
 
         early = [(0, 0), (1, 0), (2, 0), (3, 0), (0, 1), (1, 1), (2, 1)]
         for n, key in enumerate(early):
@@ -290,57 +288,71 @@ def tile_list_mlat_outl_dl_exp_kernel(
             gather_words(j0, UNIT)
             for nt in range(4):
                 vv_base(vv_bank[nt, 0][:, j0 : j0 + UNIT], 0, nt, j0, UNIT, j0 == 0)
-        gather_words(BANK, BANK)
+        for j0 in (BANK, BANK + UNIT):
+            gather_words(j0, UNIT)
         base(1, early[:4], False)
         base(1, early[4:], True)
         base(0, early[4:], False)
-        for a in range(PASSES):
-            for g, keys in enumerate(([(0, 0), (0, 1), (1, 0), (1, 1)], [(2, 0), (2, 1), (3, 0)])):
-                cast_wvd(a, g, True)
-                quantize_wvd(a, g)
-                delta(a, keys)
+        by_columns = [[(0, 0), (0, 1), (1, 0), (1, 1)], [(2, 0), (2, 1), (3, 0)]]
+        for a, g in ((0, 0), (0, 1), (1, 0)):
+            cast_wvd(a, g, True)
+            quantize_wvd(a, g)
+            delta(a, by_columns[g])
         w8_p, w4_p, w_sc = permute_w()
+        cast_wvd(1, 1, True)
+        quantize_wvd(1, 1, "w_sc_raw")
+        delta(1, by_columns[1])
+        for nt in range(3):
+            vv_store(sb("vv_res%d" % nt, [P, J], F32)[:], nt, 0, [vv_bank[nt, h][:] for h in range(2)], True)
+        for mt in range(2):
+            cast_x(0, mt, 1, False)
+        for mt in range(2):
+            quantize_x(0, mt, 1)
+        pairs = [(banks[7], vv_bank[0, 0]), (vv_bank[0, 1], vv_bank[1, 0])]
+        for mt in range(2):
+            for a in range(PASSES):
+                project_passes(mt, pairs[mt][a], a, 0, True)
+        for mt in range(2):
+            cast_x(1, mt, 1, False)
+            quantize_x(1, mt, 1)
         for a in range(PASSES):
-            cast_x(a, 0, a == 1)
-            quantize_x(a, 0)
-        vv_res = sb("vv_res", [P, 3 * J], F32, "x_raw1_0")
-        for nt in range(2):
-            vv_store(vv_res[:, nt * J : (nt + 1) * J], nt, 0, [vv_bank[nt, h][:] for h in range(2)], True)
-        for a in range(PASSES):
-            cast_x(a, 1, False)
-        for a in range(PASSES):
-            quantize_x(a, 1)
-        project(0, (banks[7], vv_bank[0, 0]), W8_FIRST)
-        copy_on(True, vv_res[:, 2 * J : 2 * J + BANK], vv_bank[2, 0][:])
-        project(1, (vv_bank[0, 1], vv_bank[1, 0]), BY_BANK)
-        copy_on(True, vv_res[:, 2 * J + BANK :], vv_bank[2, 1][:])
-        nc.sync.dma_start(out=out_1[2 * P : 3 * P, :], in_=vv_res[:, 2 * J :])
-        vv_store(sb("vv_res3", [P, BANK], F32, "x_bf1_0")[:], 3, 0, [vv_bank[3, 0][:]], False)
-        score(0, (vv_bank[1, 1], vv_bank[2, 0]), False)
+            cast_x(a, 2, 2, False)
+            quantize_x(a, 2, 2)
+        for mt in range(2):
+            for a in range(PASSES):
+                project_passes(mt, pairs[mt][a], a, 1, False)
+            quantize_qa(mt, pairs[mt], True)
+        vv_store(sb("vv_res3", [P, BANK], F32, "qa_bf0_0")[:], 3, 0, [vv_bank[3, 0][:]], False)
 
-        ring = [banks[b] for b in (3, 6, 7, 0, 4, 1, 5, 2)]
+        ring = [banks[b] for b in (5, 2, 7, 0, 6, 3, 4, 1)]
         taken = []
 
         def next_pair():
             taken.append(len(taken))
             return ring[2 * taken[-1] % 8], ring[(2 * taken[-1] + 1) % 8]
 
+        def vv_piece(bank, c0, width, on_scalar):
+            j0 = BANK + c0
+            step = min(width, UNIT)
+            for a in range(PASSES):
+                for c in range(0, width, step):
+                    n = min(step, width - c)
+                    vv_base(bank[:, c : c + n], a, 3, j0 + c, n, a == 0 and c == 0)
+            for a in range(PASSES):
+                for c in range(0, width, P):
+                    vv_delta(bank[:, c : c + P], a, 3, j0 + c, P, a == PASSES - 1 and c == width - P)
+            vv_store(sb("vv_last%d" % c0, [P, width], F32)[:], 3, j0, [bank[:, :width]], on_scalar)
+
         tiles = M // P
         for mt in range(2, tiles):
             if mt < tiles - 2:
-                a, u = mt % 2, mt // 2 + 1
-                cast_x(a, u, False)
-                quantize_x(a, u)
-            project(mt, next_pair(), BY_BANK)
-            if mt < tiles - 2:
-                score(mt - 1, next_pair(), False)
-        for mt in range(tiles - 3, tiles):
-            score(mt, next_pair(), True)
-        for n, bank in enumerate(next_pair()):
-            j0 = BANK + n * UNIT
-            for a in range(PASSES):
-                vv_base(bank[:, :UNIT], a, 3, j0, UNIT, a == 0)
-            for a in range(PASSES):
-                for c0 in (0, P):
-                    vv_delta(bank[:, c0 : c0 + P], a, 3, j0 + c0, P, a == PASSES - 1 and c0 == P)
-            vv_store(sb("vv_last%d" % n, [P, UNIT], F32)[:], 3, j0, [bank[:, :UNIT]], n == 1)
+                a, ahead = mt % 2, mt - mt % 2 + 2
+                cast_x(a, ahead, 2, False)
+                quantize_x(a, ahead, 2)
+            project(mt, next_pair())
+            score(mt - 2, next_pair(), mt == tiles - 1)
+        score(6, next_pair(), True)
+        score(7, next_pair(), True)
+        last = next_pair()
+        vv_piece(last[0], 0, 256, False)
+        vv_piece(last[1], 256, 256, True)

@@ -112,13 +112,13 @@ def tile_list_mlat_outl_dl_exp_kernel(
             load_w_scales(w8_scales, ROWS, q)
         load_wvd(0)
         load_w_scales(w8_scales, ROWS, 2)
-        nc.sync.dma_start(out=w4_raw[:].bitcast(I32), in_=w4_words[0].bitcast(I32))
         nc.vector.tensor_copy(plane0[:], tab_sc[:].indirect(offsets[:]))
         for q in range(4):
             nc.sync.dma_start(
                 out=plane1[32 * q : 32 * q + ROWS, :].bitcast(I32),
                 in_=plane0[32 * q + ROWS : 32 * q + 2 * ROWS, :].bitcast(I32),
             )
+        nc.sync.dma_start(out=w4_raw[:].bitcast(I32), in_=w4_words[0].bitcast(I32))
         load_wvd(1)
         nc.sync.dma_start(out=w8_raw[:], in_=w8_words[0].rearrange("p r b -> p (r b)").bitcast(I32))
         load_w_scales(w8_scales, ROWS, 3)
@@ -144,8 +144,8 @@ def tile_list_mlat_outl_dl_exp_kernel(
 
         parted = [sb("tab_parted%d" % h, [P, PASSES * 2 * BANK], U8) for h in range(2)]
 
-        def gather_words(j0, count):
-            both = sb("tab_both%d" % j0, [P, count], I32, "tab_both%d" % (j0 // count % 2))
+        def gather(j0, count, slot):
+            both = sb("tab_both%d" % j0, [P, count], I32, slot)
             listed = offsets[:, j0 // 16 : (j0 + count) // 16]
             nc.vector.tensor_copy(both[:].bitcast(U32), tab_w[:].bitcast(U32).indirect(listed))
             c0 = j0 % BANK
@@ -154,14 +154,14 @@ def tile_list_mlat_outl_dl_exp_kernel(
                 in_=both[:].bitcast(U16).rearrange("p (j a) -> p a j", a=PASSES),
             )
 
-        def with_table(out, codes, scales, a, j0, count, start, stop):
-            c0 = a * BANK + j0 % BANK
+        def with_table(bank, codes, scales, a, h, start, stop, c0=0, count=BANK):
+            first = a * BANK + c0
             nc.tensor.matmul_mx(
-                out=out,
+                out=bank[:, c0 : c0 + count],
                 lhsT=codes,
                 lhsT_scale=scales,
-                rhs=parted[j0 // BANK][:, 2 * c0 : 2 * (c0 + count)].bitcast(FP4X4),
-                rhs_scale=tab_planes[a][:, j0 : j0 + count],
+                rhs=parted[h][:, 2 * first : 2 * (first + count)].bitcast(FP4X4),
+                rhs_scale=tab_planes[a][:, h * BANK + c0 : h * BANK + c0 + count],
                 start=start,
                 stop=stop,
             )
@@ -170,7 +170,7 @@ def tile_list_mlat_outl_dl_exp_kernel(
         wvd_q = {}
         x_bf = {}
         x_q = {}
-        vv_bank = {}
+        vv_bank = [(banks[2 * nt], banks[2 * nt + 1]) for nt in range(N // P)]
 
         def cast_wvd(a, g, on_scalar):
             wvd_bf[a, g] = interleave("wvd_bf%d%d" % (a, g), wvd_raw[a][:, :, g * UNIT : (g + 1) * UNIT], on_scalar)
@@ -187,21 +187,23 @@ def tile_list_mlat_outl_dl_exp_kernel(
             for n in range(count):
                 x_q[a, mt + n] = codes[:, P * n : P * (n + 1)].bitcast(FP8X4), scales[:, P * n : P * (n + 1)]
 
-        def vv_base(out, a, nt, j0, count, start):
-            codes = wv4_w[:, a, 2 * P * nt : 2 * P * (nt + 1)].bitcast(FP4X4)
-            with_table(out, codes, wv4_sc[:, a, P * nt : P * (nt + 1)], a, j0, count, start, False)
+        def vv_base(a, h, start, c0=0, count=BANK):
+            for nt in range(N // P):
+                codes = wv4_w[:, a, 2 * P * nt : 2 * P * (nt + 1)].bitcast(FP4X4)
+                with_table(vv_bank[nt][h], codes, wv4_sc[:, a, P * nt : P * (nt + 1)], a, h, start, False, c0, count)
 
-        def vv_delta(out, a, nt, j0, count, stop):
-            codes, scales = wvd_q[a, nt // 2]
-            cols = slice(P * (nt % 2), P * (nt % 2 + 1))
-            with_table(out, codes[:, cols].bitcast(FP8X4), scales[:, cols], a, j0, count, False, stop)
+        def vv_delta(a, g):
+            codes, scales = wvd_q[a, g]
+            for n in range(2):
+                cols = slice(P * n, P * (n + 1))
+                for h in range(2):
+                    with_table(vv_bank[2 * g + n][h], codes[:, cols].bitcast(FP8X4), scales[:, cols], a, h, False, a == PASSES - 1)
 
-        def vv_store(res, nt, j0, parts, on_scalar):
-            c0 = 0
-            for part in parts:
-                copy_on(on_scalar, res[:, c0 : c0 + part.shape[1]], part)
-                c0 += part.shape[1]
-            nc.sync.dma_start(out=out_1[P * nt : P * (nt + 1), j0 : j0 + c0], in_=res)
+        def vv_store(nt, on_scalar, slot=None):
+            res = sb("vv_res%d" % nt, [P, J], F32, slot)
+            for h in range(2):
+                copy_on(on_scalar, res[:, h * BANK : (h + 1) * BANK], vv_bank[nt][h][:])
+            nc.sync.dma_start(out=out_1[P * nt : P * (nt + 1), :], in_=res[:])
 
         def permute_w():
             w8_p = sb("w8_p", [P, R], I32)
@@ -261,7 +263,7 @@ def tile_list_mlat_outl_dl_exp_kernel(
             order = [(a, h) for h in range(2) for a in range(PASSES)] if split_store else [(a, h) for a in range(PASSES) for h in range(2)]
             for a, h in order:
                 codes, scales = qa_q[a, mt]
-                with_table(pair[h][:], codes[:].bitcast(FP8X4), scales[:], a, h * BANK, BANK, a == 0, a == PASSES - 1)
+                with_table(pair[h], codes[:].bitcast(FP8X4), scales[:], a, h, a == 0, a == PASSES - 1)
             res = sb("sc_res%d" % mt, [P, J], F32)
             rows = slice(P * mt, P * (mt + 1))
             for h in range(2):
@@ -272,46 +274,40 @@ def tile_list_mlat_outl_dl_exp_kernel(
             if not split_store:
                 nc.sync.dma_start(out=out_0[rows, :], in_=res[:])
 
-        early = [(0, 0), (1, 0), (2, 0), (3, 0), (0, 1), (1, 1), (2, 1)]
-        for n, key in enumerate(early):
-            vv_bank[key] = banks[n]
-
-        def base(a, keys, start):
-            for nt, h in keys:
-                vv_base(vv_bank[nt, h][:], a, nt, h * BANK, BANK, start)
-
-        def delta(a, keys):
-            for nt, h in keys:
-                vv_delta(vv_bank[nt, h][:], a, nt, h * BANK, BANK, a == PASSES - 1)
-
-        for j0 in (0, UNIT):
-            gather_words(j0, UNIT)
-            for nt in range(4):
-                vv_base(vv_bank[nt, 0][:, j0 : j0 + UNIT], 0, nt, j0, UNIT, j0 == 0)
-        for j0 in (BANK, BANK + UNIT):
-            gather_words(j0, UNIT)
-        base(1, early[:4], False)
-        base(1, early[4:], True)
-        base(0, early[4:], False)
-        by_columns = [[(0, 0), (0, 1), (1, 0), (1, 1)], [(2, 0), (2, 1), (3, 0)]]
+        for n in range(3):
+            nc.tensor.matmul_mx(
+                out=banks[7][:],
+                lhsT=wv4_w[:, 0, : 2 * P].bitcast(FP4X4),
+                lhsT_scale=plane0[:, :P],
+                rhs=wv4_w[:, 0, :].bitcast(FP4X4),
+                rhs_scale=plane0[:, :BANK],
+                start=True,
+                stop=True,
+            )
+        for c0 in (0, UNIT):
+            gather(c0, UNIT, "tab_both%d" % c0)
+            vv_base(0, 0, c0 == 0, c0, UNIT)
+        vv_base(1, 0, False)
+        gather(BANK, BANK, "tab_both%d" % UNIT)
+        vv_base(1, 1, True)
+        vv_base(0, 1, False)
         for a, g in ((0, 0), (0, 1), (1, 0)):
             cast_wvd(a, g, True)
             quantize_wvd(a, g)
-            delta(a, by_columns[g])
+            vv_delta(a, g)
         w8_p, w4_p, w_sc = permute_w()
         cast_wvd(1, 1, True)
         quantize_wvd(1, 1, "w_sc_raw")
-        delta(1, by_columns[1])
+        vv_delta(1, 1)
         for nt in range(3):
-            vv_store(sb("vv_res%d" % nt, [P, J], F32)[:], nt, 0, [vv_bank[nt, h][:] for h in range(2)], True)
+            vv_store(nt, True)
         for mt in range(2):
             cast_x(0, mt, 1, False)
         for mt in range(2):
             quantize_x(0, mt, 1)
-        pairs = [(banks[7], vv_bank[0, 0]), (vv_bank[0, 1], vv_bank[1, 0])]
         for mt in range(2):
             for a in range(PASSES):
-                project_passes(mt, pairs[mt][a], a, 0, True)
+                project_passes(mt, vv_bank[mt][a], a, 0, True)
         for mt in range(2):
             cast_x(1, mt, 1, False)
             quantize_x(1, mt, 1)
@@ -320,39 +316,37 @@ def tile_list_mlat_outl_dl_exp_kernel(
             quantize_x(a, 2, 2)
         for mt in range(2):
             for a in range(PASSES):
-                project_passes(mt, pairs[mt][a], a, 1, False)
-            quantize_qa(mt, pairs[mt], True)
-        vv_store(sb("vv_res3", [P, BANK], F32, "qa_bf0_0")[:], 3, 0, [vv_bank[3, 0][:]], False)
+                project_passes(mt, vv_bank[mt][a], a, 1, False)
+            quantize_qa(mt, vv_bank[mt], True)
+        vv_store(3, False, "qa_bf0_0")
 
-        ring = [banks[b] for b in (5, 2, 7, 0, 6, 3, 4, 1)]
+        ring = [vv_bank[n] for n in (2, 0, 3, 1)]
         taken = []
 
         def next_pair():
-            taken.append(len(taken))
-            return ring[2 * taken[-1] % 8], ring[(2 * taken[-1] + 1) % 8]
-
-        def vv_piece(bank, c0, width, on_scalar):
-            j0 = BANK + c0
-            step = min(width, UNIT)
-            for a in range(PASSES):
-                for c in range(0, width, step):
-                    n = min(step, width - c)
-                    vv_base(bank[:, c : c + n], a, 3, j0 + c, n, a == 0 and c == 0)
-            for a in range(PASSES):
-                for c in range(0, width, P):
-                    vv_delta(bank[:, c : c + P], a, 3, j0 + c, P, a == PASSES - 1 and c == width - P)
-            vv_store(sb("vv_last%d" % c0, [P, width], F32)[:], 3, j0, [bank[:, :width]], on_scalar)
+            taken.append(ring[len(taken) % len(ring)])
+            return taken[-1]
 
         tiles = M // P
-        for mt in range(2, tiles):
-            if mt < tiles - 2:
-                a, ahead = mt % 2, mt - mt % 2 + 2
-                cast_x(a, ahead, 2, False)
-                quantize_x(a, ahead, 2)
-            project(mt, next_pair())
-            score(mt - 2, next_pair(), mt == tiles - 1)
+        cast_x(0, 4, 2, False)
+        quantize_x(0, 4, 2)
+        project(2, next_pair())
+        score(0, next_pair(), False)
+        cast_x(1, 4, 2, False)
+        quantize_x(1, 4, 2)
+        project(3, next_pair())
+        score(1, next_pair(), False)
+        score(2, next_pair(), False)
+        cast_x(0, 6, 2, False)
+        quantize_x(0, 6, 2)
+        project(4, next_pair())
+        score(3, next_pair(), False)
+        cast_x(1, 6, 2, False)
+        quantize_x(1, 6, 2)
+        project(5, next_pair())
+        score(4, next_pair(), False)
+        project(6, next_pair())
+        score(5, next_pair(), False)
+        project(7, next_pair())
         score(6, next_pair(), True)
         score(7, next_pair(), True)
-        last = next_pair()
-        vv_piece(last[0], 0, 256, False)
-        vv_piece(last[1], 256, 256, True)

@@ -56,9 +56,8 @@ def tile_list_mlat_outl_dl_exp_kernel(
         w4_raw = sb("w4_raw", [P, 2 * R], U8)
         w_sc_raw = sb("w_sc_raw", [P, R], U8)
 
-        nc.vector.memset(tab_sc[:, : T // 2].bitcast(I32), 0)
-        nc.gpsimd.memset(tab_sc[:, T // 2 :].bitcast(I32), 0)
-        nc.gpsimd.memset(wv4_sc[:].rearrange("p a n -> p (a n)").bitcast(I32), 0)
+        nc.vector.memset(tab_sc[:].bitcast(I32), 0)
+        nc.vector.memset(wv4_sc[:].rearrange("p a n -> p (a n)").bitcast(I32), 0)
         zero = sb("zero", [P, 1], F32)
         nc.vector.memset(w_sc_raw[:].bitcast(I32), 0)
         nc.vector.memset(plane1[:].bitcast(I32), 0)

@@ -24,6 +24,7 @@ PASSES = 2
 BANK = 512
 UNIT = 256
 ROWS = 4
+PARK = 8
 
 
 def tile_list_mlat_outl_dl_exp_kernel(
@@ -94,34 +95,42 @@ def tile_list_mlat_outl_dl_exp_kernel(
 
         plane0 = sb("plane0", [P, J], U8)
         tab_planes = [plane0, plane1]
+        def load_tab_scales(q, eng):
+            eng.dma_start(
+                out=tab_sc[32 * q : 32 * q + ROWS, :].bitcast(I32),
+                in_=tab_scales[0, ROWS * q : ROWS * (q + 1), :].bitcast(I32),
+            )
+
+        def move_rows(q, eng):
+            eng.dma_start(
+                out=plane1[32 * q : 32 * q + ROWS, :].bitcast(I32),
+                in_=plane0[PARK + ROWS * q : PARK + ROWS * (q + 1), :].bitcast(I32),
+            )
+
         nc.sync.dma_start(offsets[:], offs)
         nc.sync.dma_start(out=wv4_w[:].bitcast(I32), in_=wv4_words.rearrange("a p c -> p a c").bitcast(I32))
-        for q in range(4):
-            (nc.sync if q < 2 else nc.scalar).dma_start(
-                out=tab_sc[32 * q : 32 * q + PASSES * ROWS, :].bitcast(I32),
-                in_=tab_scales[:, ROWS * q : ROWS * (q + 1), :].bitcast(I32),
-            )
-        load_wv4_scales(0)
+        load_tab_scales(0, nc.sync)
+        load_tab_scales(2, nc.scalar)
+        load_tab_scales(1, nc.sync)
+        load_tab_scales(3, nc.scalar)
+        nc.sync.dma_start(out=tab_sc[PARK : PARK + 4 * ROWS, :].bitcast(I32), in_=tab_scales[1].bitcast(I32))
         no_bias = sb("no_bias", [P, 1], F32)
         nc.scalar.activation(out=no_bias[:], in_=zero[:], func=COPY)
         nc.sync.dma_start(out=tab_w[:], in_=tab_words[0].rearrange("p t b -> p (t b)").bitcast(I32))
-        for q in range(1, 4):
+        for q in (0, 2, 1, 3):
             load_wv4_scales(q)
-        for q in range(2):
-            load_w_scales(w8_scales, ROWS, q)
+        load_w_scales(w8_scales, ROWS, 0)
         load_wvd(0)
         load_w_scales(w8_scales, ROWS, 2)
         nc.vector.tensor_copy(plane0[:], tab_sc[:].indirect(offsets[:]))
-        for q in range(4):
-            nc.sync.dma_start(
-                out=plane1[32 * q : 32 * q + ROWS, :].bitcast(I32),
-                in_=plane0[32 * q + ROWS : 32 * q + 2 * ROWS, :].bitcast(I32),
-            )
-        nc.sync.dma_start(out=w4_raw[:].bitcast(I32), in_=w4_words[0].bitcast(I32))
+        for q in (0, 2, 1, 3):
+            move_rows(q, nc.sync)
         load_wvd(1)
-        nc.sync.dma_start(out=w8_raw[:], in_=w8_words[0].rearrange("p r b -> p (r b)").bitcast(I32))
+        load_w_scales(w8_scales, ROWS, 1)
         load_w_scales(w8_scales, ROWS, 3)
-        for q in range(4):
+        nc.sync.dma_start(out=w4_raw[:].bitcast(I32), in_=w4_words[0].bitcast(I32))
+        nc.sync.dma_start(out=w8_raw[:], in_=w8_words[0].rearrange("p r b -> p (r b)").bitcast(I32))
+        for q in (0, 2, 1, 3):
             load_w_scales(w4_scales, 0, q)
         for a, u0, count in ((0, 0, 2), (1, 0, 1), (1, 1, 1), (0, 2, 2), (1, 2, 1), (1, 3, 1)):
             load_x(a, u0, count)

@@ -25,6 +25,7 @@ BANK = 512
 UNIT = 256
 ROWS = 4
 PARK = 8
+PAIRED = 4
 
 
 def tile_list_mlat_outl_dl_exp_kernel(
@@ -72,14 +73,14 @@ def tile_list_mlat_outl_dl_exp_kernel(
 
         def load_wv4_scales(q):
             nc.sync.dma_start(
-                out=wv4_sc[32 * q : 32 * q + ROWS].bitcast(I32),
-                in_=wv4_scales[:, ROWS * q : ROWS * (q + 1), :].rearrange("a r c -> r a c").bitcast(I32),
+                out=wv4_sc[q:P:32].bitcast(I32),
+                in_=wv4_scales[:, q::ROWS, :].rearrange("a r c -> r a c").bitcast(I32),
             )
 
         def load_w_scales(src, row, q):
             nc.sync.dma_start(
-                out=w_sc_raw[32 * q + row : 32 * q + row + ROWS, :].bitcast(I32),
-                in_=src[0, ROWS * q : ROWS * (q + 1), :].bitcast(I32),
+                out=w_sc_raw[row + q : P : 32, :].bitcast(I32),
+                in_=src[0, q::ROWS, :].bitcast(I32),
             )
 
         wvd_raw = {}
@@ -97,14 +98,14 @@ def tile_list_mlat_outl_dl_exp_kernel(
         tab_planes = [plane0, plane1]
         def load_tab_scales(q, eng):
             eng.dma_start(
-                out=tab_sc[32 * q : 32 * q + ROWS, :].bitcast(I32),
-                in_=tab_scales[0, ROWS * q : ROWS * (q + 1), :].bitcast(I32),
+                out=tab_sc[q:P:32, :].bitcast(I32),
+                in_=tab_scales[0, q::ROWS, :].bitcast(I32),
             )
 
         def move_rows(q, eng):
             eng.dma_start(
-                out=plane1[32 * q : 32 * q + ROWS, :].bitcast(I32),
-                in_=plane0[PARK + ROWS * q : PARK + ROWS * (q + 1), :].bitcast(I32),
+                out=plane1[q:P:32, :].bitcast(I32),
+                in_=plane0[PARK + q : PARK + 4 * ROWS : ROWS, :].bitcast(I32),
             )
 
         nc.sync.dma_start(offsets[:], offs)
@@ -234,6 +235,7 @@ def tile_list_mlat_outl_dl_exp_kernel(
             return w8_p, w4_p, w_sc
 
         qa_q = {}
+        paired = {}
 
         def project_passes(mt, bank, a, kp, first):
             for i in range(PACK):
@@ -272,14 +274,23 @@ def tile_list_mlat_outl_dl_exp_kernel(
             for a, h in order:
                 codes, scales = qa_q[a, mt]
                 with_table(pair[h], codes[:].bitcast(FP8X4), scales[:], a, h, a == 0, a == PASSES - 1)
-            res = sb("sc_res%d" % mt, [P, J], F32)
+            if mt < PAIRED:
+                if mt % 2 == 0:
+                    paired[mt // 2] = sb("sc_res%d" % mt, [P, 2, J], F32)
+                res = paired[mt // 2][:, mt % 2, :]
+            else:
+                res = sb("sc_res%d" % mt, [P, J], F32)
             rows = slice(P * mt, P * (mt + 1))
             for h in range(2):
                 cols = slice(h * BANK, (h + 1) * BANK)
                 nc.scalar.activation(out=res[:, cols], in_=pair[h][:], func=EXP, bias=no_bias[:], scale=SCORE_SCALE)
                 if split_store:
                     nc.sync.dma_start(out=out_0[rows, cols], in_=res[:, cols])
-            if not split_store:
+            if mt < PAIRED:
+                if mt % 2 == 1:
+                    both = out_0[P * (mt - 1) : P * (mt + 1), :].rearrange("(t p) j -> p t j", p=P)
+                    nc.sync.dma_start(out=both, in_=paired[mt // 2][:])
+            elif not split_store:
                 nc.sync.dma_start(out=out_0[rows, :], in_=res[:])
 
         for n in range(3):
@@ -307,8 +318,11 @@ def tile_list_mlat_outl_dl_exp_kernel(
         cast_wvd(1, 1, True)
         quantize_wvd(1, 1, "w_sc_raw")
         vv_delta(1, 1)
+        res = sb("vv_res", [P, 3, J], F32)
         for nt in range(3):
-            vv_store(nt, True)
+            for h in range(2):
+                copy_on(True, res[:, nt, h * BANK : (h + 1) * BANK], vv_bank[nt][h][:])
+        nc.sync.dma_start(out=out_1[: 3 * P, :].rearrange("(t p) j -> p t j", p=P), in_=res[:])
         for mt in range(2):
             cast_x(0, mt, 1, False)
         for mt in range(2):

@@ -126,18 +126,19 @@ def tile_list_mlat_outl_dl_exp_kernel(
         nc.vector.tensor_copy(plane0[:], tab_sc[:].indirect(offsets[:]))
         for q in (0, 2, 1, 3):
             move_rows(q, nc.sync)
-        load_wvd(1)
         load_w_scales(w8_scales, ROWS, 1)
+        load_wvd(1)
         load_w_scales(w8_scales, ROWS, 3)
-        nc.sync.dma_start(out=w4_raw[:].bitcast(I32), in_=w4_words[0].bitcast(I32))
-        nc.sync.dma_start(out=w8_raw[:], in_=w8_words[0].rearrange("p r b -> p (r b)").bitcast(I32))
         for q in (0, 2, 1, 3):
             load_w_scales(w4_scales, 0, q)
-        for a, u0, count in ((0, 0, 2), (1, 0, 1), (1, 1, 1), (0, 2, 2), (1, 2, 1), (1, 3, 1)):
+        nc.sync.dma_start(out=w8_raw[:], in_=w8_words[0].rearrange("p r b -> p (r b)").bitcast(I32))
+        load_x(0, 0, 2)
+        nc.sync.dma_start(out=w4_raw[:].bitcast(I32), in_=w4_words[0].bitcast(I32))
+        for a, u0, count in ((1, 0, 1), (1, 1, 1), (0, 2, 2), (1, 2, 1), (1, 3, 1)):
             load_x(a, u0, count)
 
-        def interleave(name, raw, on_scalar):
-            grouped = sb(name, [P, raw.shape[2] * PACK], BF16)
+        def interleave(name, raw, on_scalar, slot=None):
+            grouped = sb(name, [P, raw.shape[2] * PACK], BF16, slot)
             copy_on(
                 on_scalar,
                 grouped[:].rearrange("p (c j i) -> p c i j", j=4, i=PACK),
@@ -187,9 +188,9 @@ def tile_list_mlat_outl_dl_exp_kernel(
         def quantize_wvd(a, g, slot=None):
             wvd_q[a, g] = quantize("wvd%d%d" % (a, g), wvd_bf[a, g], UNIT, slot)
 
-        def cast_x(a, mt, count, on_scalar):
+        def cast_x(a, mt, count, on_scalar, slot=None):
             c0 = P * (mt % 2)
-            x_bf[a, mt] = interleave("x_bf%d_%d" % (a, mt), x_raw[a, mt // 2][:, :, c0 : c0 + count * P], on_scalar)
+            x_bf[a, mt] = interleave("x_bf%d_%d" % (a, mt), x_raw[a, mt // 2][:, :, c0 : c0 + count * P], on_scalar, slot)
 
         def quantize_x(a, mt, count):
             codes, scales = quantize("x%d_%d" % (a, mt), x_bf[a, mt], count * P)
@@ -224,10 +225,6 @@ def tile_list_mlat_outl_dl_exp_kernel(
                     out=w8_p[:, cols].rearrange("p (i c j) -> p c i j", i=PACK, j=4),
                     in_=w8_raw[:, cols].rearrange("p (c j i) -> p c i j", i=PACK, j=4),
                 )
-            nc.vector.tensor_copy(
-                out=w4_p[:].bitcast(U16).rearrange("p (a i m) -> p a i m", a=PASSES, i=PACK),
-                in_=w4_raw[:].bitcast(U16).rearrange("p (a m i) -> p a i m", a=PASSES, i=PACK),
-            )
             nc.vector.tensor_copy(
                 out=w_sc[:].rearrange("p (a i m) -> p a i m", a=PASSES, i=PACK),
                 in_=w_sc_raw[:].rearrange("p (a m i) -> p a i m", a=PASSES, i=PACK),
@@ -285,7 +282,8 @@ def tile_list_mlat_outl_dl_exp_kernel(
                 cols = slice(h * BANK, (h + 1) * BANK)
                 nc.scalar.activation(out=res[:, cols], in_=pair[h][:], func=EXP, bias=no_bias[:], scale=SCORE_SCALE)
                 if split_store:
-                    nc.sync.dma_start(out=out_0[rows, cols], in_=res[:, cols])
+                    queue = nc.scalar if mt == M // P - 1 and h == 1 else nc.sync
+                    queue.dma_start(out=out_0[rows, cols], in_=res[:, cols])
             if mt < PAIRED:
                 if mt % 2 == 1:
                     both = out_0[P * (mt - 1) : P * (mt + 1), :].rearrange("(t p) j -> p t j", p=P)
@@ -293,13 +291,13 @@ def tile_list_mlat_outl_dl_exp_kernel(
             elif not split_store:
                 nc.sync.dma_start(out=out_0[rows, :], in_=res[:])
 
-        for n in range(3):
+        for plane in (tab_sc, tab_sc, tab_sc, plane0, plane0):
             nc.tensor.matmul_mx(
                 out=banks[7][:],
                 lhsT=wv4_w[:, 0, : 2 * P].bitcast(FP4X4),
-                lhsT_scale=plane0[:, :P],
+                lhsT_scale=plane[:, :P],
                 rhs=wv4_w[:, 0, :].bitcast(FP4X4),
-                rhs_scale=plane0[:, :BANK],
+                rhs_scale=plane[:, :BANK],
                 start=True,
                 stop=True,
             )
@@ -307,9 +305,10 @@ def tile_list_mlat_outl_dl_exp_kernel(
             gather(c0, UNIT, "tab_both%d" % c0)
             vv_base(0, 0, c0 == 0, c0, UNIT)
         vv_base(1, 0, False)
-        gather(BANK, BANK, "tab_both%d" % UNIT)
-        vv_base(1, 1, True)
-        vv_base(0, 1, False)
+        for c0 in (0, UNIT):
+            gather(BANK + c0, UNIT, "tab_both%d" % c0)
+            vv_base(1, 1, c0 == 0, c0, UNIT)
+            vv_base(0, 1, False, c0, UNIT)
         for a, g in ((0, 0), (0, 1), (1, 0)):
             cast_wvd(a, g, True)
             quantize_wvd(a, g)
@@ -327,19 +326,29 @@ def tile_list_mlat_outl_dl_exp_kernel(
             cast_x(0, mt, 1, False)
         for mt in range(2):
             quantize_x(0, mt, 1)
+        nc.vector.tensor_copy(
+            out=w4_p[:].bitcast(U16).rearrange("p (a i m) -> p a i m", a=PASSES, i=PACK),
+            in_=w4_raw[:].bitcast(U16).rearrange("p (a m i) -> p a i m", a=PASSES, i=PACK),
+        )
         for mt in range(2):
             for a in range(PASSES):
                 project_passes(mt, vv_bank[mt][a], a, 0, True)
         for mt in range(2):
             cast_x(1, mt, 1, False)
+        for mt in range(2):
             quantize_x(1, mt, 1)
         for a in range(PASSES):
-            cast_x(a, 2, 2, False)
-            quantize_x(a, 2, 2)
+            cast_x(a, 2, 1, False, "x_bf1_0" if a == 0 else None)
+        for a in range(PASSES):
+            quantize_x(a, 2, 1)
         for mt in range(2):
             for a in range(PASSES):
                 project_passes(mt, vv_bank[mt][a], a, 1, False)
             quantize_qa(mt, vv_bank[mt], True)
+        for a in range(PASSES):
+            cast_x(a, 3, 1, False, "x_bf1_1" if a == 0 else None)
+        for a in range(PASSES):
+            quantize_x(a, 3, 1)
         vv_store(3, False, "qa_bf0_0")
 
         ring = [vv_bank[n] for n in (2, 0, 3, 1)]

@@ -377,7 +377,7 @@ def tile_list_mlat_outl_dl_exp_kernel(
         project(5, next_pair())
         score(4, next_pair(), False)
         project(6, next_pair())
-        score(5, next_pair(), False)
         project(7, next_pair())
+        score(5, next_pair(), True)
         score(6, next_pair(), True)
         score(7, next_pair(), True)

@@ -109,7 +109,7 @@ def tile_list_mlat_outl_dl_exp_kernel(
             )
 
         nc.sync.dma_start(offsets[:], offs)
-        nc.sync.dma_start(out=wv4_w[:].bitcast(I32), in_=wv4_words.rearrange("a p c -> p a c").bitcast(I32))
+        nc.sync.dma_start(out=wv4_w[:, 0, :].bitcast(I32), in_=wv4_words[0].bitcast(I32))
         load_tab_scales(0, nc.sync)
         load_tab_scales(2, nc.scalar)
         load_tab_scales(1, nc.sync)
@@ -120,20 +120,22 @@ def tile_list_mlat_outl_dl_exp_kernel(
         nc.sync.dma_start(out=tab_w[:], in_=tab_words[0].rearrange("p t b -> p (t b)").bitcast(I32))
         for q in (0, 2, 1, 3):
             load_wv4_scales(q)
-        load_w_scales(w8_scales, ROWS, 0)
+        nc.sync.dma_start(out=wv4_w[:, 1, :].bitcast(I32), in_=wv4_words[1].bitcast(I32))
         load_wvd(0)
         load_w_scales(w8_scales, ROWS, 2)
         nc.vector.tensor_copy(plane0[:], tab_sc[:].indirect(offsets[:]))
         for q in (0, 2, 1, 3):
             move_rows(q, nc.sync)
-        load_w_scales(w8_scales, ROWS, 1)
+        load_w_scales(w8_scales, ROWS, 0)
         load_wvd(1)
-        load_w_scales(w8_scales, ROWS, 3)
-        for q in (0, 2, 1, 3):
+        for q in (1, 3):
+            load_w_scales(w8_scales, ROWS, q)
+        for q in (0, 2, 1):
             load_w_scales(w4_scales, 0, q)
         nc.sync.dma_start(out=w8_raw[:], in_=w8_words[0].rearrange("p r b -> p (r b)").bitcast(I32))
-        load_x(0, 0, 2)
         nc.sync.dma_start(out=w4_raw[:].bitcast(I32), in_=w4_words[0].bitcast(I32))
+        load_w_scales(w4_scales, 0, 3)
+        load_x(0, 0, 2)
         for a, u0, count in ((1, 0, 1), (1, 1, 1), (0, 2, 2), (1, 2, 1), (1, 3, 1)):
             load_x(a, u0, count)
 
@@ -158,10 +160,14 @@ def tile_list_mlat_outl_dl_exp_kernel(
             both = sb("tab_both%d" % j0, [P, count], I32, slot)
             listed = offsets[:, j0 // 16 : (j0 + count) // 16]
             nc.vector.tensor_copy(both[:].bitcast(U32), tab_w[:].bitcast(U32).indirect(listed))
+            return both
+
+        def part(both, j0, first, last):
             c0 = j0 % BANK
+            dst = parted[j0 // BANK][:].bitcast(U16).rearrange("p (a j) -> p a j", a=PASSES)
             nc.vector.tensor_copy(
-                out=parted[j0 // BANK][:].bitcast(U16).rearrange("p (a j) -> p a j", a=PASSES)[:, :, c0 : c0 + count],
-                in_=both[:].bitcast(U16).rearrange("p (j a) -> p a j", a=PASSES),
+                out=dst[:, first:last, c0 : c0 + UNIT],
+                in_=both[:].bitcast(U16).rearrange("p (j a) -> p a j", a=PASSES)[:, first:last, :],
             )
 
         def with_table(bank, codes, scales, a, h, start, stop, c0=0, count=BANK):
@@ -301,12 +307,16 @@ def tile_list_mlat_outl_dl_exp_kernel(
                 start=True,
                 stop=True,
             )
+        early = {}
         for c0 in (0, UNIT):
-            gather(c0, UNIT, "tab_both%d" % c0)
+            early[c0] = gather(c0, UNIT, "tab_both%d" % c0)
+            part(early[c0], c0, 0, 1)
             vv_base(0, 0, c0 == 0, c0, UNIT)
+        for c0 in (0, UNIT):
+            part(early[c0], c0, 1, 2)
         vv_base(1, 0, False)
         for c0 in (0, UNIT):
-            gather(BANK + c0, UNIT, "tab_both%d" % c0)
+            part(gather(BANK + c0, UNIT, "tab_both%d" % c0), BANK + c0, 0, 2)
             vv_base(1, 1, c0 == 0, c0, UNIT)
             vv_base(0, 1, False, c0, UNIT)
         for a, g in ((0, 0), (0, 1), (1, 0)):

@@ -38,7 +38,7 @@ def tile_list_mlat_outl_dl_exp_kernel(
         psum = ctx.enter_context(tc.psum_pool(name="psum", bufs=1))
 
         def sb(name, shape, dtype, slot=None):
-            return keep.tile(shape, dtype, name=name, tag=slot or name, align_bytes=64)
+            return keep.tile(shape, dtype, name=name, tag=slot or name, align_bytes=256)
 
         banks = [psum.tile([P, BANK], F32, name="bank%d" % b) for b in range(8)]
 

@@ -26,6 +26,7 @@ UNIT = 256
 ROWS = 4
 PARK = 8
 PAIRED = 4
+MOVING_CODES, STILL_SCALES, MOVING_SCALES = 128, 64, 192
 
 
 def tile_list_mlat_outl_dl_exp_kernel(
@@ -40,6 +41,9 @@ def tile_list_mlat_outl_dl_exp_kernel(
         def sb(name, shape, dtype, slot=None):
             return keep.tile(shape, dtype, name=name, tag=slot or name, align_bytes=256)
 
+        def placed(name, cols, dtype, size, phase, slot=None):
+            return sb(name, [P, phase // size + cols], dtype, slot)[:, phase // size :]
+
         banks = [psum.tile([P, BANK], F32, name="bank%d" % b) for b in range(8)]
 
         def copy_on(on_scalar, dst, src):
@@ -51,7 +55,7 @@ def tile_list_mlat_outl_dl_exp_kernel(
         offsets = lists.tile([P, J // 16], U16, name="offsets")
         tab_sc = sb("tab_sc", [P, T], U8)
         tab_w = sb("tab_w", [P, T], I32)
-        plane1 = sb("plane1", [P, J], U8)
+        plane1 = placed("plane1", J, U8, 1, MOVING_SCALES)
         wv4_w = sb("wv4_w", [P, PASSES, 2 * N], U8)
         wv4_sc = sb("wv4_sc", [P, PASSES, N], U8)
         w8_raw = sb("w8_raw", [P, R], I32)
@@ -94,7 +98,7 @@ def tile_list_mlat_outl_dl_exp_kernel(
             for n in range(count):
                 x_raw[a, u0 + n] = raw[:, :, n * UNIT : (n + 1) * UNIT]
 
-        plane0 = sb("plane0", [P, J], U8)
+        plane0 = placed("plane0", J, U8, 1, MOVING_SCALES)
         tab_planes = [plane0, plane1]
         def load_tab_scales(q, eng):
             eng.dma_start(
@@ -148,13 +152,13 @@ def tile_list_mlat_outl_dl_exp_kernel(
             )
             return grouped
 
-        def quantize(name, grouped, cols, slot=None):
-            codes = sb(name + "_codes", [P, cols], U32, slot)
-            scales = sb(name + "_scales", [P, cols], U8)
+        def quantize(name, grouped, cols, moving, slot=None):
+            codes = placed(name + "_codes", cols, U32, 4, MOVING_CODES if moving else 0, slot)
+            scales = placed(name + "_scales", cols, U8, 1, MOVING_SCALES if moving else STILL_SCALES)
             nc.vector.quantize_mx(out=codes[:].bitcast(FP8X4), scales=scales[:], in_=grouped[:])
             return codes, scales
 
-        parted = [sb("tab_parted%d" % h, [P, PASSES * 2 * BANK], U8) for h in range(2)]
+        parted = [placed("tab_parted%d" % h, PASSES * 2 * BANK, U8, 1, MOVING_CODES) for h in range(2)]
 
         def gather(j0, count, slot):
             both = sb("tab_both%d" % j0, [P, count], I32, slot)
@@ -192,14 +196,14 @@ def tile_list_mlat_outl_dl_exp_kernel(
             wvd_bf[a, g] = interleave("wvd_bf%d%d" % (a, g), wvd_raw[a][:, :, g * UNIT : (g + 1) * UNIT], on_scalar)
 
         def quantize_wvd(a, g, slot=None):
-            wvd_q[a, g] = quantize("wvd%d%d" % (a, g), wvd_bf[a, g], UNIT, slot)
+            wvd_q[a, g] = quantize("wvd%d%d" % (a, g), wvd_bf[a, g], UNIT, False, slot)
 
         def cast_x(a, mt, count, on_scalar, slot=None):
             c0 = P * (mt % 2)
             x_bf[a, mt] = interleave("x_bf%d_%d" % (a, mt), x_raw[a, mt // 2][:, :, c0 : c0 + count * P], on_scalar, slot)
 
         def quantize_x(a, mt, count):
-            codes, scales = quantize("x%d_%d" % (a, mt), x_bf[a, mt], count * P)
+            codes, scales = quantize("x%d_%d" % (a, mt), x_bf[a, mt], count * P, True)
             for n in range(count):
                 x_q[a, mt + n] = codes[:, P * n : P * (n + 1)].bitcast(FP8X4), scales[:, P * n : P * (n + 1)]
 
@@ -224,7 +228,7 @@ def tile_list_mlat_outl_dl_exp_kernel(
         def permute_w():
             w8_p = sb("w8_p", [P, R], I32)
             w4_p = sb("w4_p", [P, 2 * R], U8)
-            w_sc = sb("w_sc", [P, R], U8)
+            w_sc = placed("w_sc", R, U8, 1, STILL_SCALES)
             for a in range(PASSES):
                 cols = slice(a * K_PASS, (a + 1) * K_PASS)
                 nc.vector.tensor_copy(
@@ -265,7 +269,7 @@ def tile_list_mlat_outl_dl_exp_kernel(
                 copy_on(a == 0 or both_on_scalar, qa_bf[:].rearrange("p (m i) -> p m i", i=PACK), pair[a][:].rearrange("p (i m) -> p m i", i=PACK))
                 grouped.append(qa_bf)
             for a in range(PASSES):
-                qa_q[a, mt] = quantize("qa%d_%d" % (a, mt), grouped[a], P)
+                qa_q[a, mt] = quantize("qa%d_%d" % (a, mt), grouped[a], P, False)
 
         def project(mt, pair):
             for a, kp, first in ((0, 0, True), (0, 1, False), (1, 1, True), (1, 0, False)):

@@ -125,19 +125,18 @@ def tile_list_mlat_outl_dl_exp_kernel(
         for q in (0, 2, 1, 3):
             load_wv4_scales(q)
         nc.sync.dma_start(out=wv4_w[:, 1, :].bitcast(I32), in_=wv4_words[1].bitcast(I32))
-        load_wvd(0)
-        load_w_scales(w8_scales, ROWS, 2)
+        nc.sync.dma_start(out=w8_raw[:], in_=w8_words[0].rearrange("p r b -> p (r b)").bitcast(I32))
+        nc.sync.dma_start(out=w4_raw[:].bitcast(I32), in_=w4_words[0].bitcast(I32))
+        load_w_scales(w8_scales, ROWS, 0)
         nc.vector.tensor_copy(plane0[:], tab_sc[:].indirect(offsets[:]))
         for q in (0, 2, 1, 3):
             move_rows(q, nc.sync)
-        load_w_scales(w8_scales, ROWS, 0)
-        load_wvd(1)
-        for q in (1, 3):
+        load_wvd(0)
+        for q in (2, 1, 3):
             load_w_scales(w8_scales, ROWS, q)
         for q in (0, 2, 1):
             load_w_scales(w4_scales, 0, q)
-        nc.sync.dma_start(out=w8_raw[:], in_=w8_words[0].rearrange("p r b -> p (r b)").bitcast(I32))
-        nc.sync.dma_start(out=w4_raw[:].bitcast(I32), in_=w4_words[0].bitcast(I32))
+        load_wvd(1)
         load_w_scales(w4_scales, 0, 3)
         load_x(0, 0, 2)
         for a, u0, count in ((1, 0, 1), (1, 1, 1), (0, 2, 2), (1, 2, 1), (1, 3, 1)):
@@ -225,21 +224,28 @@ def tile_list_mlat_outl_dl_exp_kernel(
                 copy_on(on_scalar, res[:, h * BANK : (h + 1) * BANK], vv_bank[nt][h][:])
             nc.sync.dma_start(out=out_1[P * nt : P * (nt + 1), :], in_=res[:])
 
-        def permute_w():
-            w8_p = sb("w8_p", [P, R], I32)
+        def deal_words():
+            w8_p = sb("w8_p", [P, R], U32)
             w4_p = sb("w4_p", [P, 2 * R], U8)
-            w_sc = placed("w_sc", R, U8, 1, STILL_SCALES)
             for a in range(PASSES):
                 cols = slice(a * K_PASS, (a + 1) * K_PASS)
-                nc.vector.tensor_copy(
+                nc.scalar.copy(
                     out=w8_p[:, cols].rearrange("p (i c j) -> p c i j", i=PACK, j=4),
-                    in_=w8_raw[:, cols].rearrange("p (c j i) -> p c i j", i=PACK, j=4),
+                    in_=w8_raw[:, cols].bitcast(U32).rearrange("p (c j i) -> p c i j", i=PACK, j=4),
                 )
+            nc.scalar.copy(
+                out=w4_p[:].bitcast(U16).rearrange("p (a i m) -> p a i m", a=PASSES, i=PACK),
+                in_=w4_raw[:].bitcast(U16).rearrange("p (a m i) -> p a i m", a=PASSES, i=PACK),
+            )
+            return w8_p, w4_p
+
+        def deal_scales():
+            w_sc = placed("w_sc", R, U8, 1, STILL_SCALES, "wvd_bf11")
             nc.vector.tensor_copy(
                 out=w_sc[:].rearrange("p (a i m) -> p a i m", a=PASSES, i=PACK),
                 in_=w_sc_raw[:].rearrange("p (a m i) -> p a i m", a=PASSES, i=PACK),
             )
-            return w8_p, w4_p, w_sc
+            return w_sc
 
         qa_q = {}
         paired = {}
@@ -323,14 +329,14 @@ def tile_list_mlat_outl_dl_exp_kernel(
             part(gather(BANK + c0, UNIT, "tab_both%d" % c0), BANK + c0, 0, 2)
             vv_base(1, 1, c0 == 0, c0, UNIT)
             vv_base(0, 1, False, c0, UNIT)
-        for a, g in ((0, 0), (0, 1), (1, 0)):
-            cast_wvd(a, g, True)
-            quantize_wvd(a, g)
-            vv_delta(a, g)
-        w8_p, w4_p, w_sc = permute_w()
-        cast_wvd(1, 1, True)
-        quantize_wvd(1, 1, "w_sc_raw")
-        vv_delta(1, 1)
+        w8_p, w4_p = deal_words()
+        for a in range(PASSES):
+            for g in range(2):
+                cast_wvd(a, g, g == 1)
+            for g in range(2):
+                quantize_wvd(a, g)
+                vv_delta(a, g)
+        w_sc = deal_scales()
         res = sb("vv_res", [P, 3, J], F32)
         for nt in range(3):
             for h in range(2):
@@ -340,10 +346,6 @@ def tile_list_mlat_outl_dl_exp_kernel(
             cast_x(0, mt, 1, False)
         for mt in range(2):
             quantize_x(0, mt, 1)
-        nc.vector.tensor_copy(
-            out=w4_p[:].bitcast(U16).rearrange("p (a i m) -> p a i m", a=PASSES, i=PACK),
-            in_=w4_raw[:].bitcast(U16).rearrange("p (a m i) -> p a i m", a=PASSES, i=PACK),
-        )
         for mt in range(2):
             for a in range(PASSES):
                 project_passes(mt, vv_bank[mt][a], a, 0, True)

@@ -124,22 +124,20 @@ def tile_list_mlat_outl_dl_exp_kernel(
         nc.sync.dma_start(out=tab_w[:], in_=tab_words[0].rearrange("p t b -> p (t b)").bitcast(I32))
         for q in (0, 2, 1, 3):
             load_wv4_scales(q)
+        load_w_scales(w8_scales, ROWS, 0)
         nc.sync.dma_start(out=wv4_w[:, 1, :].bitcast(I32), in_=wv4_words[1].bitcast(I32))
         nc.sync.dma_start(out=w8_raw[:], in_=w8_words[0].rearrange("p r b -> p (r b)").bitcast(I32))
         nc.sync.dma_start(out=w4_raw[:].bitcast(I32), in_=w4_words[0].bitcast(I32))
-        load_w_scales(w8_scales, ROWS, 0)
         nc.vector.tensor_copy(plane0[:], tab_sc[:].indirect(offsets[:]))
         for q in (0, 2, 1, 3):
             move_rows(q, nc.sync)
+        load_w_scales(w4_scales, 0, 0)
         load_wvd(0)
         for q in (2, 1, 3):
             load_w_scales(w8_scales, ROWS, q)
-        for q in (0, 2, 1):
             load_w_scales(w4_scales, 0, q)
         load_wvd(1)
-        load_w_scales(w4_scales, 0, 3)
-        load_x(0, 0, 2)
-        for a, u0, count in ((1, 0, 1), (1, 1, 1), (0, 2, 2), (1, 2, 1), (1, 3, 1)):
+        for a, u0, count in ((0, 0, 1), (1, 0, 1), (0, 1, 1), (1, 1, 1), (0, 2, 2), (1, 2, 1), (1, 3, 1)):
             load_x(a, u0, count)
 
         def interleave(name, raw, on_scalar, slot=None):
@@ -191,11 +189,13 @@ def tile_list_mlat_outl_dl_exp_kernel(
         x_q = {}
         vv_bank = [(banks[2 * nt], banks[2 * nt + 1]) for nt in range(N // P)]
 
-        def cast_wvd(a, g, on_scalar):
-            wvd_bf[a, g] = interleave("wvd_bf%d%d" % (a, g), wvd_raw[a][:, :, g * UNIT : (g + 1) * UNIT], on_scalar)
+        def cast_wvd(a, nt, count, on_scalar):
+            wvd_bf[a, nt] = interleave("wvd_bf%d%d" % (a, nt), wvd_raw[a][:, :, nt * P : (nt + count) * P], on_scalar)
 
-        def quantize_wvd(a, g, slot=None):
-            wvd_q[a, g] = quantize("wvd%d%d" % (a, g), wvd_bf[a, g], UNIT, False, slot)
+        def quantize_wvd(a, nt, count):
+            codes, scales = quantize("wvd%d%d" % (a, nt), wvd_bf[a, nt], count * P, False)
+            for n in range(count):
+                wvd_q[a, nt + n] = codes[:, P * n : P * (n + 1)].bitcast(FP8X4), scales[:, P * n : P * (n + 1)]
 
         def cast_x(a, mt, count, on_scalar, slot=None):
             c0 = P * (mt % 2)
@@ -211,12 +211,10 @@ def tile_list_mlat_outl_dl_exp_kernel(
                 codes = wv4_w[:, a, 2 * P * nt : 2 * P * (nt + 1)].bitcast(FP4X4)
                 with_table(vv_bank[nt][h], codes, wv4_sc[:, a, P * nt : P * (nt + 1)], a, h, start, False, c0, count)
 
-        def vv_delta(a, g):
-            codes, scales = wvd_q[a, g]
-            for n in range(2):
-                cols = slice(P * n, P * (n + 1))
-                for h in range(2):
-                    with_table(vv_bank[2 * g + n][h], codes[:, cols].bitcast(FP8X4), scales[:, cols], a, h, False, a == PASSES - 1)
+        def vv_delta(a, nt):
+            codes, scales = wvd_q[a, nt]
+            for h in range(2):
+                with_table(vv_bank[nt][h], codes, scales, a, h, False, a == PASSES - 1)
 
         def vv_store(nt, on_scalar, slot=None):
             res = sb("vv_res%d" % nt, [P, J], F32, slot)
@@ -239,13 +237,14 @@ def tile_list_mlat_outl_dl_exp_kernel(
             )
             return w8_p, w4_p
 
-        def deal_scales():
-            w_sc = placed("w_sc", R, U8, 1, STILL_SCALES, "wvd_bf11")
+        w_sc = {}
+
+        def deal_scales(a, slot):
+            w_sc[a] = placed("w_sc%d" % a, K_PASS, U8, 1, STILL_SCALES, slot)
             nc.vector.tensor_copy(
-                out=w_sc[:].rearrange("p (a i m) -> p a i m", a=PASSES, i=PACK),
-                in_=w_sc_raw[:].rearrange("p (a m i) -> p a i m", a=PASSES, i=PACK),
+                out=w_sc[a][:].rearrange("p (b i m) -> p b i m", b=2, i=2),
+                in_=w_sc_raw[:, a * K_PASS : (a + 1) * K_PASS].rearrange("p (m b i) -> p b i m", b=2, i=2),
             )
-            return w_sc
 
         qa_q = {}
         paired = {}
@@ -254,9 +253,9 @@ def tile_list_mlat_outl_dl_exp_kernel(
             for i in range(PACK):
                 c = a * K_PASS + i * P
                 if kp == 0:
-                    w_codes, w_plane = w8_p[:, c : c + P].bitcast(FP8X4), w_sc[ROWS:P, c : c + P]
+                    w_codes, w_plane = w8_p[:, c : c + P].bitcast(FP8X4), w_sc[a][ROWS:P, i * P : (i + 1) * P]
                 else:
-                    w_codes, w_plane = w4_p[:, 2 * c : 2 * (c + P)].bitcast(FP4X4), w_sc[:, c : c + P]
+                    w_codes, w_plane = w4_p[:, 2 * c : 2 * (c + P)].bitcast(FP4X4), w_sc[a][:, i * P : (i + 1) * P]
                 x_codes, x_plane = x_q[kp, mt]
                 nc.tensor.matmul_mx(
                     out=bank[:, i * P : (i + 1) * P],
@@ -272,13 +271,17 @@ def tile_list_mlat_outl_dl_exp_kernel(
             grouped = []
             for a in range(PASSES):
                 qa_bf = sb("qa_bf%d_%d" % (a, mt), [P, K_PASS], BF16)
-                copy_on(a == 0 or both_on_scalar, qa_bf[:].rearrange("p (m i) -> p m i", i=PACK), pair[a][:].rearrange("p (i m) -> p m i", i=PACK))
+                copy_on((a == 0 and mt < 6) or both_on_scalar, qa_bf[:].rearrange("p (m i) -> p m i", i=PACK), pair[a][:].rearrange("p (i m) -> p m i", i=PACK))
                 grouped.append(qa_bf)
             for a in range(PASSES):
                 qa_q[a, mt] = quantize("qa%d_%d" % (a, mt), grouped[a], P, False)
 
         def project(mt, pair):
-            for a, kp, first in ((0, 0, True), (0, 1, False), (1, 1, True), (1, 0, False)):
+            if mt == 2:
+                order = ((0, 0, True), (1, 0, True), (0, 1, False), (1, 1, False))
+            else:
+                order = ((0, 0, True), (0, 1, False), (1, 1, True), (1, 0, False))
+            for a, kp, first in order:
                 project_passes(mt, pair[a], a, kp, first)
             quantize_qa(mt, pair, False)
 
@@ -331,12 +334,19 @@ def tile_list_mlat_outl_dl_exp_kernel(
             vv_base(0, 1, False, c0, UNIT)
         w8_p, w4_p = deal_words()
         for a in range(PASSES):
-            for g in range(2):
-                cast_wvd(a, g, g == 1)
-            for g in range(2):
-                quantize_wvd(a, g)
-                vv_delta(a, g)
-        w_sc = deal_scales()
+            for nt in range(2):
+                cast_wvd(a, nt, 1, False)
+            cast_wvd(a, 2, 2, True)
+            for nt in range(2):
+                quantize_wvd(a, nt, 1)
+                vv_delta(a, nt)
+            if a == 1:
+                deal_scales(1, "wvd_bf11")
+            quantize_wvd(a, 2, 2)
+            for nt in (2, 3):
+                vv_delta(a, nt)
+            if a == 0:
+                deal_scales(0, "wvd_bf02")
         res = sb("vv_res", [P, 3, J], F32)
         for nt in range(3):
             for h in range(2):
@@ -354,7 +364,7 @@ def tile_list_mlat_outl_dl_exp_kernel(
         for mt in range(2):
             quantize_x(1, mt, 1)
         for a in range(PASSES):
-            cast_x(a, 2, 1, False, "x_bf1_0" if a == 0 else None)
+            cast_x(a, 2, 1, False)
         for a in range(PASSES):
             quantize_x(a, 2, 1)
         for mt in range(2):
@@ -367,7 +377,7 @@ def tile_list_mlat_outl_dl_exp_kernel(
             quantize_x(a, 3, 1)
         vv_store(3, False, "qa_bf0_0")
 
-        ring = [vv_bank[n] for n in (2, 0, 3, 1)]
+        ring = [vv_bank[n] for n in (2, 0, 1, 3)]
         taken = []
 
         def next_pair():
@@ -375,18 +385,22 @@ def tile_list_mlat_outl_dl_exp_kernel(
             return taken[-1]
 
         tiles = M // P
-        cast_x(0, 4, 2, False)
-        quantize_x(0, 4, 2)
         project(2, next_pair())
         score(0, next_pair(), False)
-        cast_x(1, 4, 2, False)
-        quantize_x(1, 4, 2)
+        for a in range(PASSES):
+            cast_x(a, 4, 1, False)
+        for a in range(PASSES):
+            quantize_x(a, 4, 1)
         project(3, next_pair())
         score(1, next_pair(), False)
         score(2, next_pair(), False)
-        cast_x(0, 6, 2, False)
-        quantize_x(0, 6, 2)
+        for a in range(PASSES):
+            cast_x(a, 5, 1, False, "qa_bf%d_3" % a)
+        for a in range(PASSES):
+            quantize_x(a, 5, 1)
         project(4, next_pair())
+        cast_x(0, 6, 2, False, "qa_bf0_4")
+        quantize_x(0, 6, 2)
         score(3, next_pair(), False)
         cast_x(1, 6, 2, False)
         quantize_x(1, 6, 2)

@@ -271,7 +271,7 @@ def tile_list_mlat_outl_dl_exp_kernel(
             grouped = []
             for a in range(PASSES):
                 qa_bf = sb("qa_bf%d_%d" % (a, mt), [P, K_PASS], BF16)
-                copy_on((a == 0 and mt < 6) or both_on_scalar, qa_bf[:].rearrange("p (m i) -> p m i", i=PACK), pair[a][:].rearrange("p (i m) -> p m i", i=PACK))
+                copy_on((a == 0 and mt < 5) or both_on_scalar, qa_bf[:].rearrange("p (m i) -> p m i", i=PACK), pair[a][:].rearrange("p (i m) -> p m i", i=PACK))
                 grouped.append(qa_bf)
             for a in range(PASSES):
                 qa_q[a, mt] = quantize("qa%d_%d" % (a, mt), grouped[a], P, False)
@@ -286,7 +286,7 @@ def tile_list_mlat_outl_dl_exp_kernel(
             quantize_qa(mt, pair, False)
 
         def score(mt, pair, split_store):
-            order = [(a, h) for h in range(2) for a in range(PASSES)] if split_store else [(a, h) for a in range(PASSES) for h in range(2)]
+            order = [(a, h) for h in range(2) for a in range(PASSES)] if mt > 0 else [(a, h) for a in range(PASSES) for h in range(2)]
             for a, h in order:
                 codes, scales = qa_q[a, mt]
                 with_table(pair[h], codes[:].bitcast(FP8X4), scales[:], a, h, a == 0, a == PASSES - 1)

from contextlib import ExitStack

import concourse.mybir as mybir

K, R, M, T, N, J = 1024, 1024, 1024, 2048, 512, 1024
FLOPS = 2 * K * R * M + 2 * R * M * J + 2 * 2 * R * N * J
SCORE_SCALE = 0.015625

F32 = mybir.dt.float32
BF16 = mybir.dt.bfloat16
I32 = mybir.dt.int32
U32 = mybir.dt.uint32
U16 = mybir.dt.uint16
U8 = mybir.dt.uint8
FP8X4 = mybir.dt.float8_e4m3fn_x4
FP4X4 = mybir.dt.float4_e2m1fn_x4
COPY = mybir.ActivationFunctionType.Copy
EXP = mybir.ActivationFunctionType.Exp

P = 128
PACK = 4
K_PASS = P * PACK
PASSES = 2
BANK = 512
UNIT = 256
ROWS = 4
PARK = 8
PAIRED = 4
MOVING_CODES, STILL_SCALES, MOVING_SCALES = 128, 64, 192


def tile_list_mlat_outl_dl_exp_kernel(
    tc, x, w8_words, w8_scales, w4_words, w4_scales, tab_words, tab_scales, wv4_words, wv4_scales, wvd, offs, out_0, out_1
):
    nc = tc.nc
    with ExitStack() as ctx:
        lists = ctx.enter_context(tc.tile_pool(name="lists", bufs=1))
        keep = ctx.enter_context(tc.tile_pool(name="keep", bufs=1))
        psum = ctx.enter_context(tc.psum_pool(name="psum", bufs=1))

        def sb(name, shape, dtype, slot=None):
            return keep.tile(shape, dtype, name=name, tag=slot or name, align_bytes=256)

        def placed(name, cols, dtype, size, phase, slot=None):
            return sb(name, [P, phase // size + cols], dtype, slot)[:, phase // size :]

        banks = [psum.tile([P, BANK], F32, name="bank%d" % b) for b in range(8)]

        def copy_on(on_scalar, dst, src):
            if on_scalar:
                nc.scalar.activation(out=dst, in_=src, func=COPY)
            else:
                nc.vector.tensor_copy(out=dst, in_=src)

        offsets = lists.tile([P, J // 16], U16, name="offsets")
        tab_sc = sb("tab_sc", [P, T], U8)
        tab_w = sb("tab_w", [P, T], I32)
        plane1 = placed("plane1", J, U8, 1, MOVING_SCALES)
        wv4_w = sb("wv4_w", [P, PASSES, 2 * N], U8)
        wv4_sc = sb("wv4_sc", [P, PASSES, N], U8)
        w8_raw = sb("w8_raw", [P, R], I32)
        w4_raw = sb("w4_raw", [P, 2 * R], U8)
        w_sc_raw = sb("w_sc_raw", [P, R], U8)

        nc.vector.memset(tab_sc[:].bitcast(I32), 0)
        nc.vector.memset(wv4_sc[:].rearrange("p a n -> p (a n)").bitcast(I32), 0)
        zero = sb("zero", [P, 1], F32)
        nc.vector.memset(w_sc_raw[:].bitcast(I32), 0)
        nc.vector.memset(plane1[:].bitcast(I32), 0)
        nc.vector.memset(zero[:], 0.0)

        def load_rows(name, src, a, c0, width):
            raw = sb(name, [P, PACK, width], F32, name)
            rows = src[a * K_PASS : (a + 1) * K_PASS, c0 : c0 + width]
            nc.sync.dma_start(out=raw[:], in_=rows.rearrange("(p i) c -> p i c", i=PACK))
            return raw

        def load_wv4_scales(q):
            nc.sync.dma_start(
                out=wv4_sc[q:P:32].bitcast(I32),
                in_=wv4_scales[:, q::ROWS, :].rearrange("a r c -> r a c").bitcast(I32),
            )

        def load_w_scales(src, row, q):
            nc.sync.dma_start(
                out=w_sc_raw[row + q : P : 32, :].bitcast(I32),
                in_=src[0, q::ROWS, :].bitcast(I32),
            )

        wvd_raw = {}
        x_raw = {}

        def load_wvd(a):
            wvd_raw[a] = load_rows("wvd_raw%d" % a, wvd, a, 0, N)

        def load_x(a, u0, count):
            raw = load_rows("x_raw%d_%d" % (a, u0), x, a, u0 * UNIT, count * UNIT)
            for n in range(count):
                x_raw[a, u0 + n] = raw[:, :, n * UNIT : (n + 1) * UNIT]

        plane0 = placed("plane0", J, U8, 1, MOVING_SCALES)
        tab_planes = [plane0, plane1]
        def load_tab_scales(q, eng):
            eng.dma_start(
                out=tab_sc[q:P:32, :].bitcast(I32),
                in_=tab_scales[0, q::ROWS, :].bitcast(I32),
            )

        def move_rows(q, eng):
            eng.dma_start(
                out=plane1[q:P:32, :].bitcast(I32),
                in_=plane0[PARK + q : PARK + 4 * ROWS : ROWS, :].bitcast(I32),
            )

        nc.sync.dma_start(offsets[:], offs)
        nc.sync.dma_start(out=wv4_w[:, 0, :].bitcast(I32), in_=wv4_words[0].bitcast(I32))
        load_tab_scales(0, nc.sync)
        load_tab_scales(2, nc.scalar)
        load_tab_scales(1, nc.sync)
        load_tab_scales(3, nc.scalar)
        nc.sync.dma_start(out=tab_sc[PARK : PARK + 4 * ROWS, :].bitcast(I32), in_=tab_scales[1].bitcast(I32))
        no_bias = sb("no_bias", [P, 1], F32)
        nc.scalar.activation(out=no_bias[:], in_=zero[:], func=COPY)
        nc.sync.dma_start(out=tab_w[:], in_=tab_words[0].rearrange("p t b -> p (t b)").bitcast(I32))
        for q in (0, 2, 1, 3):
            load_wv4_scales(q)
        load_w_scales(w8_scales, ROWS, 0)
        nc.sync.dma_start(out=wv4_w[:, 1, :].bitcast(I32), in_=wv4_words[1].bitcast(I32))
        nc.sync.dma_start(out=w8_raw[:], in_=w8_words[0].rearrange("p r b -> p (r b)").bitcast(I32))
        nc.sync.dma_start(out=w4_raw[:].bitcast(I32), in_=w4_words[0].bitcast(I32))
        nc.vector.tensor_copy(plane0[:], tab_sc[:].indirect(offsets[:]))
        for q in (0, 2, 1, 3):
            move_rows(q, nc.sync)
        load_w_scales(w4_scales, 0, 0)
        load_wvd(0)
        for q in (2, 1, 3):
            load_w_scales(w8_scales, ROWS, q)
            load_w_scales(w4_scales, 0, q)
        load_wvd(1)
        for a, u0, count in ((0, 0, 1), (1, 0, 1), (0, 1, 1), (1, 1, 1), (0, 2, 2), (1, 2, 1), (1, 3, 1)):
            load_x(a, u0, count)

        def interleave(name, raw, on_scalar, slot=None):
            grouped = sb(name, [P, raw.shape[2] * PACK], BF16, slot)
            copy_on(
                on_scalar,
                grouped[:].rearrange("p (c j i) -> p c i j", j=4, i=PACK),
                raw.rearrange("p i (c j) -> p c i j", j=4),
            )
            return grouped

        def quantize(name, grouped, cols, moving, slot=None):
            codes = placed(name + "_codes", cols, U32, 4, MOVING_CODES if moving else 0, slot)
            scales = placed(name + "_scales", cols, U8, 1, MOVING_SCALES if moving else STILL_SCALES)
            nc.vector.quantize_mx(out=codes[:].bitcast(FP8X4), scales=scales[:], in_=grouped[:])
            return codes, scales

        parted = [placed("tab_parted%d" % h, PASSES * 2 * BANK, U8, 1, MOVING_CODES) for h in range(2)]

        def gather(j0, count, slot):
            both = sb("tab_both%d" % j0, [P, count], I32, slot)
            listed = offsets[:, j0 // 16 : (j0 + count) // 16]
            nc.vector.tensor_copy(both[:].bitcast(U32), tab_w[:].bitcast(U32).indirect(listed))
            return both

        def part(both, j0, first, last):
            c0 = j0 % BANK
            dst = parted[j0 // BANK][:].bitcast(U16).rearrange("p (a j) -> p a j", a=PASSES)
            nc.vector.tensor_copy(
                out=dst[:, first:last, c0 : c0 + UNIT],
                in_=both[:].bitcast(U16).rearrange("p (j a) -> p a j", a=PASSES)[:, first:last, :],
            )

        def with_table(bank, codes, scales, a, h, start, stop, c0=0, count=BANK):
            first = a * BANK + c0
            nc.tensor.matmul_mx(
                out=bank[:, c0 : c0 + count],
                lhsT=codes,
                lhsT_scale=scales,
                rhs=parted[h][:, 2 * first : 2 * (first + count)].bitcast(FP4X4),
                rhs_scale=tab_planes[a][:, h * BANK + c0 : h * BANK + c0 + count],
                start=start,
                stop=stop,
            )

        wvd_bf = {}
        wvd_q = {}
        x_bf = {}
        x_q = {}
        vv_bank = [(banks[2 * nt], banks[2 * nt + 1]) for nt in range(N // P)]

        def cast_wvd(a, nt, count, on_scalar):
            wvd_bf[a, nt] = interleave("wvd_bf%d%d" % (a, nt), wvd_raw[a][:, :, nt * P : (nt + count) * P], on_scalar)

        def quantize_wvd(a, nt, count):
            codes, scales = quantize("wvd%d%d" % (a, nt), wvd_bf[a, nt], count * P, False)
            for n in range(count):
                wvd_q[a, nt + n] = codes[:, P * n : P * (n + 1)].bitcast(FP8X4), scales[:, P * n : P * (n + 1)]

        def cast_x(a, mt, count, on_scalar, slot=None):
            c0 = P * (mt % 2)
            x_bf[a, mt] = interleave("x_bf%d_%d" % (a, mt), x_raw[a, mt // 2][:, :, c0 : c0 + count * P], on_scalar, slot)

        def quantize_x(a, mt, count):
            codes, scales = quantize("x%d_%d" % (a, mt), x_bf[a, mt], count * P, True)
            for n in range(count):
                x_q[a, mt + n] = codes[:, P * n : P * (n + 1)].bitcast(FP8X4), scales[:, P * n : P * (n + 1)]

        def vv_base(a, h, start, c0=0, count=BANK):
            for nt in range(N // P):
                codes = wv4_w[:, a, 2 * P * nt : 2 * P * (nt + 1)].bitcast(FP4X4)
                with_table(vv_bank[nt][h], codes, wv4_sc[:, a, P * nt : P * (nt + 1)], a, h, start, False, c0, count)

        def vv_delta(a, nt):
            codes, scales = wvd_q[a, nt]
            for h in range(2):
                with_table(vv_bank[nt][h], codes, scales, a, h, False, a == PASSES - 1)

        def vv_store(nt, on_scalar, slot=None):
            res = sb("vv_res%d" % nt, [P, J], F32, slot)
            for h in range(2):
                copy_on(on_scalar, res[:, h * BANK : (h + 1) * BANK], vv_bank[nt][h][:])
            nc.sync.dma_start(out=out_1[P * nt : P * (nt + 1), :], in_=res[:])

        def deal_words():
            w8_p = sb("w8_p", [P, R], U32)
            w4_p = sb("w4_p", [P, 2 * R], U8)
            for a in range(PASSES):
                cols = slice(a * K_PASS, (a + 1) * K_PASS)
                nc.scalar.copy(
                    out=w8_p[:, cols].rearrange("p (i c j) -> p c i j", i=PACK, j=4),
                    in_=w8_raw[:, cols].bitcast(U32).rearrange("p (c j i) -> p c i j", i=PACK, j=4),
                )
            nc.scalar.copy(
                out=w4_p[:].bitcast(U16).rearrange("p (a i m) -> p a i m", a=PASSES, i=PACK),
                in_=w4_raw[:].bitcast(U16).rearrange("p (a m i) -> p a i m", a=PASSES, i=PACK),
            )
            return w8_p, w4_p

        w_sc = {}

        def deal_scales(a, slot):
            w_sc[a] = placed("w_sc%d" % a, K_PASS, U8, 1, STILL_SCALES, slot)
            nc.vector.tensor_copy(
                out=w_sc[a][:].rearrange("p (b i m) -> p b i m", b=2, i=2),
                in_=w_sc_raw[:, a * K_PASS : (a + 1) * K_PASS].rearrange("p (m b i) -> p b i m", b=2, i=2),
            )

        qa_q = {}
        paired = {}

        def project_passes(mt, bank, a, kp, first):
            for i in range(PACK):
                c = a * K_PASS + i * P
                if kp == 0:
                    w_codes, w_plane = w8_p[:, c : c + P].bitcast(FP8X4), w_sc[a][ROWS:P, i * P : (i + 1) * P]
                else:
                    w_codes, w_plane = w4_p[:, 2 * c : 2 * (c + P)].bitcast(FP4X4), w_sc[a][:, i * P : (i + 1) * P]
                x_codes, x_plane = x_q[kp, mt]
                nc.tensor.matmul_mx(
                    out=bank[:, i * P : (i + 1) * P],
                    lhsT=w_codes,
                    lhsT_scale=w_plane,
                    rhs=x_codes,
                    rhs_scale=x_plane,
                    start=(first and i == 0),
                    stop=(not first and i == PACK - 1),
                )

        def quantize_qa(mt, pair, both_on_scalar):
            grouped = []
            for a in range(PASSES):
                qa_bf = sb("qa_bf%d_%d" % (a, mt), [P, K_PASS], BF16)
                copy_on((a == 0 and mt < 5) or both_on_scalar, qa_bf[:].rearrange("p (m i) -> p m i", i=PACK), pair[a][:].rearrange("p (i m) -> p m i", i=PACK))
                grouped.append(qa_bf)
            for a in range(PASSES):
                qa_q[a, mt] = quantize("qa%d_%d" % (a, mt), grouped[a], P, False)

        def project(mt, pair):
            if mt == 2:
                order = ((0, 0, True), (1, 0, True), (0, 1, False), (1, 1, False))
            else:
                order = ((0, 0, True), (0, 1, False), (1, 1, True), (1, 0, False))
            for a, kp, first in order:
                project_passes(mt, pair[a], a, kp, first)
            quantize_qa(mt, pair, False)

        def score(mt, pair, split_store):
            order = [(a, h) for h in range(2) for a in range(PASSES)] if mt > 0 else [(a, h) for a in range(PASSES) for h in range(2)]
            for a, h in order:
                codes, scales = qa_q[a, mt]
                with_table(pair[h], codes[:].bitcast(FP8X4), scales[:], a, h, a == 0, a == PASSES - 1)
            if mt < PAIRED:
                if mt % 2 == 0:
                    paired[mt // 2] = sb("sc_res%d" % mt, [P, 2, J], F32)
                res = paired[mt // 2][:, mt % 2, :]
            else:
                res = sb("sc_res%d" % mt, [P, J], F32)
            rows = slice(P * mt, P * (mt + 1))
            for h in range(2):
                cols = slice(h * BANK, (h + 1) * BANK)
                nc.scalar.activation(out=res[:, cols], in_=pair[h][:], func=EXP, bias=no_bias[:], scale=SCORE_SCALE)
                if split_store:
                    queue = nc.scalar if mt == M // P - 1 and h == 1 else nc.sync
                    queue.dma_start(out=out_0[rows, cols], in_=res[:, cols])
            if mt < PAIRED:
                if mt % 2 == 1:
                    both = out_0[P * (mt - 1) : P * (mt + 1), :].rearrange("(t p) j -> p t j", p=P)
                    nc.sync.dma_start(out=both, in_=paired[mt // 2][:])
            elif not split_store:
                nc.sync.dma_start(out=out_0[rows, :], in_=res[:])

        for plane in (tab_sc, tab_sc, tab_sc, plane0, plane0):
            nc.tensor.matmul_mx(
                out=banks[7][:],
                lhsT=wv4_w[:, 0, : 2 * P].bitcast(FP4X4),
                lhsT_scale=plane[:, :P],
                rhs=wv4_w[:, 0, :].bitcast(FP4X4),
                rhs_scale=plane[:, :BANK],
                start=True,
                stop=True,
            )
        early = {}
        for c0 in (0, UNIT):
            early[c0] = gather(c0, UNIT, "tab_both%d" % c0)
            part(early[c0], c0, 0, 1)
            vv_base(0, 0, c0 == 0, c0, UNIT)
        for c0 in (0, UNIT):
            part(early[c0], c0, 1, 2)
        vv_base(1, 0, False)
        for c0 in (0, UNIT):
            part(gather(BANK + c0, UNIT, "tab_both%d" % c0), BANK + c0, 0, 2)
            vv_base(1, 1, c0 == 0, c0, UNIT)
            vv_base(0, 1, False, c0, UNIT)
        w8_p, w4_p = deal_words()
        for a in range(PASSES):
            for nt in range(2):
                cast_wvd(a, nt, 1, False)
            cast_wvd(a, 2, 2, True)
            for nt in range(2):
                quantize_wvd(a, nt, 1)
                vv_delta(a, nt)
            if a == 1:
                deal_scales(1, "wvd_bf11")
            quantize_wvd(a, 2, 2)
            for nt in (2, 3):
                vv_delta(a, nt)
            if a == 0:
                deal_scales(0, "wvd_bf02")
        res = sb("vv_res", [P, 3, J], F32)
        for nt in range(3):
            for h in range(2):
                copy_on(True, res[:, nt, h * BANK : (h + 1) * BANK], vv_bank[nt][h][:])
        nc.sync.dma_start(out=out_1[: 3 * P, :].rearrange("(t p) j -> p t j", p=P), in_=res[:])
        for mt in range(2):
            cast_x(0, mt, 1, False)
        for mt in range(2):
            quantize_x(0, mt, 1)
        for mt in range(2):
            for a in range(PASSES):
                project_passes(mt, vv_bank[mt][a], a, 0, True)
        for mt in range(2):
            cast_x(1, mt, 1, False)
        for mt in range(2):
            quantize_x(1, mt, 1)
        for a in range(PASSES):
            cast_x(a, 2, 1, False)
        for a in range(PASSES):
            quantize_x(a, 2, 1)
        for mt in range(2):
            for a in range(PASSES):
                project_passes(mt, vv_bank[mt][a], a, 1, False)
            quantize_qa(mt, vv_bank[mt], True)
        for a in range(PASSES):
            cast_x(a, 3, 1, False, "x_bf1_1" if a == 0 else None)
        for a in range(PASSES):
            quantize_x(a, 3, 1)
        vv_store(3, False, "qa_bf0_0")

        ring = [vv_bank[n] for n in (2, 0, 1, 3)]
        taken = []

        def next_pair():
            taken.append(ring[len(taken) % len(ring)])
            return taken[-1]

        tiles = M // P
        project(2, next_pair())
        score(0, next_pair(), False)
        for a in range(PASSES):
            cast_x(a, 4, 1, False)
        for a in range(PASSES):
            quantize_x(a, 4, 1)
        project(3, next_pair())
        score(1, next_pair(), False)
        score(2, next_pair(), False)
        for a in range(PASSES):
            cast_x(a, 5, 1, False, "qa_bf%d_3" % a)
        for a in range(PASSES):
            quantize_x(a, 5, 1)
        project(4, next_pair())
        cast_x(0, 6, 2, False, "qa_bf0_4")
        quantize_x(0, 6, 2)
        score(3, next_pair(), False)
        cast_x(1, 6, 2, False)
        quantize_x(1, 6, 2)
        project(5, next_pair())
        score(4, next_pair(), False)
        project(6, next_pair())
        project(7, next_pair())
        score(5, next_pair(), True)
        score(6, next_pair(), True)
        score(7, next_pair(), True)
